import numpy as np, ml_dtypes
CORES = [242,247,114,119]
N = 4
BF = ml_dtypes.bfloat16
def gentries(a):
    return np.ascontiguousarray(a.reshape(8, 16, -1).transpose(0, 2, 1)).reshape(8, -1)
def gtable(e):
    e = np.asarray(e); return np.ascontiguousarray(e.reshape(8, -1, 16).transpose(0, 2, 1)).reshape(128, -1).astype(np.int32)
W, P, S, V, Q, F = 3072, 192, 16, 6, 16, 2048
def parts(rng):
    return (rng.integers(0, 256, (N, 8, 16, W)), rng.integers(0, W, (N, 8, P, S)), rng.integers(0, W, (N, 8, P, S)), rng.integers(0, S + 1, (N, 8, P)),
            rng.integers(0, S + 1, (N, 8, P)), rng.integers(600, 1201, (N, 8, P)), rng.integers(0, 16, (N, 8, 16)))
def first(h, m):
    return np.where(m > 0, h[..., 0], (37 * np.arange(P)) & (F - 1))
def pack(x, h, t, m, n, th, w):
    return {"x0": np.ascontiguousarray(x.reshape(N, 128, W)).astype(np.float32).astype(BF), "hands": np.stack([gtable(a.reshape(8, -1)) for a in h]), "trains": np.stack([gtable(a.reshape(8, -1)) for a in t]),
            "mh": m.astype(np.int32), "nt": n.astype(np.int32), "th": th.astype(np.int32), "wt": np.ascontiguousarray(w.reshape(N, 128, 1)).astype(np.int32)}
def setup_inputs(rng):
    return pack(*parts(rng))
def setup_inputs_spread(rng):
    x, h, t, m, n, th, w = parts(rng)
    x = np.minimum((np.exp2(8 * rng.random((N, 8, 1, W))) * rng.random((N, 8, 16, W))).astype(np.int64), 255)
    h = np.minimum((W * rng.random(h.shape) ** 3).astype(np.int64), W - 1); t = W - 1 - np.minimum((W * rng.random(t.shape) ** 2).astype(np.int64), W - 1)
    m = np.minimum(((S + 1) * rng.random(m.shape) ** 2).astype(np.int64), S); n = S - np.minimum(((S + 1) * rng.random(n.shape) ** 2).astype(np.int64), S)
    th = np.minimum(np.exp2(12 * rng.random(th.shape)).astype(np.int64) - 1, 4080)
    return pack(x, h, t, m, n, th, w)
def setup_inputs_ends(rng):
    x, h, t, m, n, th, w = parts(rng); e = W - 1; q = N - 1
    x = 255 * rng.integers(0, 2, (N, 8, 16, W)); x = np.where(rng.random((N, 8, 1, W)) < 0.25, x[:, :, :1, :], x)
    for g, b in enumerate((0, 1, 2, 1, 0, 2, 1, 0)):
        if b < 2: x[:, g, :, 0] = 255 * b
    x[:, :, :, e] = 255 - x[:, :, :, 0]
    h = np.where(rng.random(h.shape) < 0.8, e * rng.integers(0, 2, h.shape), h); t = np.where(rng.random(t.shape) < 0.8, e * rng.integers(0, 2, t.shape), t)
    m = np.where(rng.random(m.shape) < 0.85, S * rng.integers(0, 2, m.shape), m); n = np.where(rng.random(n.shape) < 0.85, S * rng.integers(0, 2, n.shape), n)
    th = np.where(rng.random(th.shape) < 0.8, 4080 * rng.integers(0, 2, th.shape), np.maximum(255 * rng.integers(0, 17, th.shape) - rng.integers(0, 2, th.shape), 0))
    w = 15 * rng.integers(0, 2, w.shape); w[:, 0] = 15; w[:, 7] = 15; w[:, 3] = 0
    a = rng.integers(0, 2, (8, P - 8))
    h[q, :, 8:, 0] = e * a; t[q, :, 8:, 0] = e * a; t[q, :, 8:, 1:] = (e * (1 - a))[:, :, None]
    m[q, :, 8:] = S; n[q, :, 8:] = S; th[q, :, 8:] = 0
    th[q, :, 2] = 4080; n[q, :, 2] = S; m[q, :, 3] = 0; n[q, :, 3] = 0
    h[q, 7, P - 1, 0] = e; n[q, 7, P - 1] = 0
    h[q, 7, 1, 0] = e; t[q, 7, 1] = 0; m[q, 7, 1] = S; n[q, 7, 1] = S; th[q, 7, 1] = 0
    return pack(x, h, t, m, n, th, w)
def setup_inputs_corners(rng):
    x, h, t, m, n, th, w = parts(rng)
    kd = rng.integers(0, 10, (N, 8, P)); kd[:, :, :10] = np.arange(10); kd[:, :, P - 10:] = np.arange(10)
    kd[0] = rng.choice(np.array([1, 4, 6]), (8, P)); kd[1] = rng.choice(np.array([0, 2, 3]), (8, P))
    kd[0, 2, 5] = 5; kd[0, 7, P - 1] = 0
    m = np.array([0, 0, S, S, 1, 1, S, 2, S - 1, 3])[kd]; n = np.array([0, S, 0, S, S, S - 1, S, S, S, 1])[kd]
    c = np.where(m > 0, h[..., 0], (37 * np.arange(P)) & (F - 1))
    t = (c[..., None] + rng.integers(1, W, t.shape)) % W; s = np.arange(S); k = kd[..., None]
    own = (((k == 1) | (k == 4) | (k == 5) | (k == 6)) & (s == 0)) | ((k == 7) & (s == S - 1)) | ((k == 8) & ((s == 3) | (s == 5))) | (k == 9)
    t = np.where(own, c[..., None], t)
    th = np.where((kd == 0) | (kd == 2), rng.choice(np.array([0, 1, 4079, 4080]), th.shape), 0)
    w[:, 1] = 0; w[:, 3] = 15; w[:, 5] = 0; w[:, 5, 15] = 1; w[:, 6] = 0; w[:, 6, 0] = 15
    return pack(x, h, t, m, n, th, w)
def setup_inputs_ties(rng):
    x, h, t, m, n, th, w = parts(rng)
    x = 4 * rng.integers(0, 64, (N, 8, 1, W)) + np.zeros((1, 1, 16, 1), np.int64)
    x[:, ::2] = x[:, ::2] + rng.integers(0, 2, (N, 4, 16, W)) * (rng.random((N, 4, 1, W)) < 0.25)
    th = np.maximum(64 * rng.integers(0, 12, th.shape) + rng.integers(-1, 2, th.shape), 0)
    t[:, 1::2] = np.where(rng.random((N, 4, P, S)) < 0.15, h[:, 1::2, :, :1], t[:, 1::2])
    t[:, 2] = rng.choice(np.array([0, 1, W - 2, W - 1]), (N, P, S)); h[:, 4] = rng.choice(np.array([0, 7, W - 1]), (N, P, S)); t[:, 6] = t[:, 6, :, :1]
    a = np.maximum(n[1], 1).reshape(-1); a[rng.permutation(8 * P)[:256]] = 0; n[1] = a.reshape(8, P)
    t[1] = np.where(np.arange(S) == n[1][..., None] - 1, first(h[1], m[1])[..., None], t[1])
    return pack(x, h, t, m, n, th, w)
def setup_inputs_counts(rng):
    x, h, t, m, n, th, w = parts(rng); b = N - 1; D = min(N - 3, V - 2, 3); p = b - D; s = np.arange(S)
    x[:2, 7] = np.where(np.arange(W) % 2 == 0, rng.integers(250, 256, (2, 16, W)), rng.integers(0, 10, (2, 16, W))); w[0, 7] = 15
    m[0, 1] = 0; n[0] = S
    m[1, 2] = 0; n[1] = np.maximum(n[1], 1); n[1, 2] = 0; n[1, 3, rng.permutation(P)[:99]] = 0
    c = first(h, m)
    t[:2] = (c[:2, ..., None] + 1 + 2 * rng.integers(0, W // 2, (2, 8, P, S))) % W
    t[0, ..., 0] = c[0]
    t[1, :7] = np.where(s == n[1, :7, :, None] - 1, c[1, :7, :, None], t[1, :7])
    XT = np.take_along_axis(x[:2], t[:2].reshape(2, 8, 1, P * S), 3).reshape(2, 8, 16, P, S); XC = np.take_along_axis(x[:2], c[:2, :, None, :], 3)
    d = np.add.reduce(np.abs(XT - XC[..., None]), axis=2)
    th[0] = np.maximum(np.min(d[0, ..., 1:], axis=-1) - 1, 0)
    th[1, 7] = np.take_along_axis(d[1, 7], n[1, 7][:, None] - 1, 1)[:, 0]
    th[p:] = 0; n[p:] = np.maximum(n[p:], 1); n[p] = S - D
    t[p:] = 8 * rng.integers(0, W // 8, (N - p, 8, P, S)); t[p, ..., 1:] = (t[p, ..., :1] + 8 * rng.integers(1, W // 8, (8, P, S - 1))) % W
    t[p:, :, P - 2:] = t[p:, :, P - 2:] + 4
    for u in range(D):
        h[p + u] = 8 * rng.integers(0, W // 8, (8, P, S)) + 1 + u; m[p + u] = rng.integers(D, S + 1, (8, P))
    h[b] = 8 * rng.integers(0, W // 8, (8, P, S)) + 7; h[b, ..., D] = np.roll(t[p, ..., 0], D, axis=0)
    m[b] = rng.integers(D + 1, S + 1, (8, P)); m[b, :, P - 2:] = 0
    return pack(x, h, t, m, n, th, w)
def check_inputs(d):
    bad = []
    for k, lo, hi in (("x0", 0, 255), ("hands", 0, W - 1), ("trains", 0, W - 1), ("mh", 0, S), ("nt", 0, S), ("th", 0, 4080), ("wt", 0, 15)):
        v = np.asarray(d[k]).astype(np.float64)
        if not (np.min(v) >= lo and np.max(v) <= hi): bad.append("range of " + k)
        elif np.any(v != np.rint(v)): bad.append("whole numbers of " + k)
    return bad
def reference(x0, hands, trains, mh, nt, th, wt):
    X = x0.astype(np.float32).astype(np.int32).reshape(N, 8, 16, W); s = np.arange(S); i = np.arange(P)
    H = np.stack([gentries(a) for a in hands]).astype(np.int64).reshape(N, 8, P, S); T = np.stack([gentries(a) for a in trains]).astype(np.int64).reshape(N, 8, P, S)
    m = mh.astype(np.int64); n = nt.astype(np.int64); lim = th.astype(np.int64); wv = wt.astype(np.int64).reshape(N, 8, 16, 1)
    H = np.where(s < m[..., None], H, 0); T = np.where(s < n[..., None], T, 0)
    A = np.zeros(N, np.int64); zero = np.zeros((N, 8, P, 1), np.int64)
    for t in range(V):
        if t > 0:
            j = 1 + t // N - (t - 1) // N
            T = np.roll(T, (1, j), axis=(0, 1)); n = np.roll(n, (1, j), axis=(0, 1))
        A3 = A[:, None, None]
        c = np.where(m > 0, H[..., 0], (37 * i + 613 * t + A3) & (F - 1))
        H = np.concatenate([H[..., 1:], zero], axis=-1); m = np.maximum(m - 1, 0)
        XT = np.take_along_axis(X, T.reshape(N, 8, 1, P * S), 3).reshape(N, 8, 16, P, S); XC = np.take_along_axis(X, c[:, :, None, :], 3)
        dist = np.add.reduce(np.abs(XT - XC[..., None]), axis=2)
        ok = (dist <= (lim + (A3 & 255))[..., None]) & (s < n[..., None])
        k = np.max(np.where(ok, s, -1), axis=-1); hit = k >= 0; got = np.where(hit, n - k, 0)
        XS = np.take_along_axis(XT, np.maximum(k, 0)[:, :, None, :, None], 4)[..., 0]
        y = np.where(hit[:, :, None, :], (XC + XS) >> 1, np.where((n == 0)[:, :, None, :], XC, np.abs(XC - XS)))
        z = np.add.reduce(wv * y, axis=2) & (Q - 1)
        np.put_along_axis(X, (Q * i + z)[:, :, None, :], y, 3)
        h1 = hit[..., None]; m1 = m[..., None]; c1 = c[..., None]; n1 = n[..., None]
        back = np.take_along_axis(T, np.clip(m1 + n1 - s, 0, S - 1), 3)
        H = np.where(h1 & (s == m1), c1, np.where(h1 & (s > m1) & (s <= m1 + got[..., None]), back, H))
        m = np.where(hit, np.minimum(m + 1 + got, S), m)
        grown = np.where(n1 == S, np.concatenate([T[..., 1:], zero], axis=-1), T)
        grown = np.where(s == np.minimum(n1, S - 1), c1, grown)
        T = np.where(h1, np.where(s < k[..., None], T, 0), grown); n = np.where(hit, k, np.minimum(n + 1, S))
        A = np.sum(got, axis=(1, 2))
    return {"yx": X.reshape(N, 128, W).astype(np.float32).astype(BF), "yh": np.stack([gtable(a.reshape(8, -1)) for a in H]).astype(np.float32), "yt": np.stack([gtable(a.reshape(8, -1)) for a in T]).astype(np.float32),
            "ym": m.astype(np.float32), "yn": n.astype(np.float32)}

@@ -1,0 +1,539 @@
+from concourse.bass import DstId, RemoteDMATransfer
+from concourse.mybir import dt, AluOpType, AxisListType, ActivationFunctionType
+import math
+
+OP = AluOpType
+AF = ActivationFunctionType
+V = 6
+NP = 192
+CW = 3088
+EMPTY = 1536.0
+PARTS = ("MX", "cols", "Wr", "b", "RW", "WIN")
+CA = 8 * 16 * (191 * 192 // 2)
+RND = 8388608.0
+
+SCRATCH = {
+    "X": ("sbuf", [128, CW], "bfloat16"),
+    "XT": ("sbuf", [128, 3072], "bfloat16"),
+    "MX": ("sbuf", [128, 3072], "bfloat16"),
+    "IOT": ("sbuf", [128, 3072], "float32"),
+    "WIN": ("sbuf", [128, 4096], "float32"),
+    "RW": ("sbuf", [128, 16 * 128], "float16"),
+    "nmi": ("sbuf", [8, 576], "int32"), "nmf": ("sbuf", [8, 576], "float32"), "R8": ("sbuf", [8, 128], "float32"),
+    "tri": ("sbuf", [128, NP], "int32"), "hai": ("sbuf", [128, NP], "int32"), "wti": ("sbuf", [128, 1], "int32"),
+    "smB": ("sbuf", [128, 272], "bfloat16"), "smC": ("sbuf", [128, 256], "bfloat16"), "smA": ("sbuf", [128, 256], "bfloat16"),
+    "cwi": ("sbuf", [128, 16], "int32"), "cwj": ("sbuf", [128, 16], "int32"), "cw": ("sbuf", [128, 16], "float32"),
+    "SC": ("sbuf", [128, 16], "float32"), "E0": ("sbuf", [128, 16], "float32"), "PC": ("sbuf", [128, 16], "float32"),
+    "WB": ("sbuf", [128, 16], "float32"), "cols": ("sbuf", [128, 16], "float32"),
+    "iq": ("sbuf", [128, 12], "float32"), "bi": ("sbuf", [128, 12], "float32"), "b16i": ("sbuf", [128, 12], "int32"),
+    "b16h": ("sbuf", [128, 12], "float16"), "b37": ("sbuf", [128, 12 * V], "float32"),
+    "onesf": ("sbuf", [128, 128], "float32"), "ones": ("sbuf", [128, NP], "bfloat16"), "oneh": ("sbuf", [128, NP], "float16"),
+    "Ib": ("sbuf", [128, 128], "bfloat16"), "NB": ("sbuf", [128, 128], "bfloat16"),
+    "W2": ("sbuf", [128, 144], "bfloat16"), "WN": ("sbuf", [128, 144], "bfloat16"), "Ww": ("sbuf", [128, 144], "bfloat16"),
+    "Wk": ("sbuf", [128, 144], "float16"), "Wr": ("sbuf", [128, 144 * V], "float16"), "W256": ("sbuf", [128, 144], "float16"),
+    "Ih": ("sbuf", [128, 256], "float16"), "SI": ("sbuf", [128, 256], "float16"), "E15": ("sbuf", [128, 256], "float16"),
+    "IN": ("sbuf", [128, 256], "float16"), "TUr": ("sbuf", [128, 256], "float16"), "BA": ("sbuf", [128, 128], "float16"),
+    "BH": ("sbuf", [128, 256], "float16"), "TUi": ("sbuf", [128, 128], "float16"), "TU8": ("sbuf", [128, 128], "float16"),
+    "I8": ("sbuf", [128, 128], "float16"), "I8n": ("sbuf", [128, 128], "float16"), "B15": ("sbuf", [128, 128], "float16"),
+    "B8n": ("sbuf", [128, 128], "float16"), "B512": ("sbuf", [128, 128], "float16"), "Bh": ("sbuf", [128, 128], "float16"),
+    "Bac": ("sbuf", [128, 128], "float16"), "B1": ("sbuf", [128, 128], "float16"), "B4k": ("sbuf", [128, 128], "float16"),
+    "B12k": ("sbuf", [128, 128], "float16"), "M8": ("sbuf", [128, 8], "float16"),
+    "thr": ("sbuf", [128, NP], "float32"), "lim": ("sbuf", [128, NP], "float32"),
+    "Th": ("sbuf", [128, NP], "float16"), "IH": ("sbuf", [128, 2 * NP], "float16"), "Hs": ("sbuf", [128, NP], "float16"),
+    "Hp": ("sbuf", [128, NP], "float16"), "ff": ("sbuf", [128, NP], "float16"), "oh": ("sbuf", [128, NP], "float16"),
+    "fT": ("sbuf", [128, NP], "float16"), "ohc": ("sbuf", [128, NP], "float16"), "crep": ("sbuf", [128, NP], "float32"),
+    "Trot": ("sbuf", [128, NP], "float32"), "xc": ("sbuf", [128, NP], "bfloat16"), "na": ("sbuf", [128, NP], "float32"),
+    "ok": ("sbuf", [128, NP], "float16"), "K1": ("sbuf", [128, NP], "float16"), "fst": ("sbuf", [128, NP], "float16"),
+    "Tc": ("sbuf", [128, NP], "float16"), "ac": ("sbuf", [128, NP], "float32"), "vv": ("sbuf", [128, NP], "float32"),
+    "uu": ("sbuf", [128, NP], "float32"), "au": ("sbuf", [128, NP], "float32"), "y": ("sbuf", [128, NP], "bfloat16"),
+    "Tcap": ("sbuf", [128, NP], "float16"), "hoc": ("sbuf", [128, NP], "float16"), "wall": ("sbuf", [128, NP], "float32"),
+    "C1": ("sbuf", [128, NP], "float32"), "Rv": ("sbuf", [128, NP], "float32"), "R2": ("sbuf", [128, NP], "float32"),
+    "R3": ("sbuf", [128, NP], "float32"),
+    "cf": ("sbuf", [128, 12], "float32"), "cl": ("sbuf", [128, 12], "uint16"), "kl": ("sbuf", [128, 12], "uint16"),
+    "zl": ("sbuf", [128, 12], "uint16"), "ql": ("sbuf", [128, 12], "uint16"),
+    "zi": ("sbuf", [128, 12], "int32"), "zj": ("sbuf", [128, 12], "int32"), "zk": ("sbuf", [128, 12], "int32"),
+    "x1": ("sbuf", [128, 12], "float32"),
+    "nd": ("sbuf", [128, 12], "float32"), "sm": ("sbuf", [128, 12 * 10], "float32"), "smi": ("sbuf", [128, 12 * 4], "int32"),
+    "aa": ("sbuf", [128, 4], "float32"), "ai": ("sbuf", [128, 2], "int32"),
+    "oyh": ("sbuf", [128, NP], "float32"), "oyt": ("sbuf", [128, NP], "float32"), "oya": ("sbuf", [128, NP], "float32"),
+    "oyb": ("sbuf", [128, NP], "float32"), "omn": ("sbuf", [8, 2 * NP], "float32"),
+}
+for _i in range(8):
+    SCRATCH["bk%d" % _i] = ("psum", [128, 512], "float32")
+for _i in range(V):
+    SCRATCH["TT%d" % _i] = ("sbuf", [128, NP], "uint16")
+for _i in range(V - 1):
+    SCRATCH["TO%d" % _i] = ("sbuf", [128, NP], "uint16")
+
+DMAS = ["dx", "dt", "dh", "dn", "dm", "dth", "dw", "ox", "oh", "ot", "om", "on"]
+SEMAPHORES = ["qV", "qA", "qP", "qG", "snd"] + ["arr%d" % i for i in range(1, V)] + ["d_" + n for n in DMAS]
+
+
+def rank_program(g, core, T, topo):
+    rank = T.rank_of(core)
+    if rank is None:
+        return
+    ops = []
+    writer, readers, bank = {}, {}, {}
+
+    def op(q, f, r=(), w=(), dma=None):
+        k = len(ops)
+        deps = set()
+        for n in r:
+            if n[:2] == "bk":
+                continue
+            if n in writer:
+                deps.add(writer[n])
+            readers.setdefault(n, []).append(k)
+        for n in w:
+            if n[:2] == "bk":
+                continue
+            if n in writer and (ops[writer[n]]["q"] != q or ops[writer[n]]["dma"] or n.rstrip("0123456789_") not in PARTS):
+                deps.add(writer[n])
+            for i in readers.get(n, []):
+                if i != k:
+                    deps.add(i)
+            writer[n] = k
+            readers[n] = []
+        for n in list(r) + list(w):
+            if n[:2] == "bk":
+                a = bank.setdefault(n, {})
+                for q2 in a:
+                    if q2 != q:
+                        deps.add(a[q2])
+                a[q] = k
+        ops.append({"q": q, "f": f, "deps": deps, "dma": dma, "inc": None})
+        return k
+
+    Q = {"V": g.vector, "A": g.scalar, "P": g.tensor, "G": g, "S": g.sync}
+
+    def ts(out, in0, s1, o1, s2, o2, r, w):
+        if o2 is None:
+            op("V", lambda: g.vector.tensor_scalar(out, in0, s1, None, o1), r, w)
+        else:
+            op("V", lambda: g.vector.tensor_scalar(out, in0, s1, s2, o1, o2), r, w)
+
+    def tt(out, a, b, o, r, w):
+        op("V", lambda: g.vector.tensor_tensor(out, a, b, o), r, w)
+
+    def cp(out, a, r, w):
+        op("V", lambda: g.vector.tensor_copy(out, a), r, w)
+
+    def act(out, a, fn, r, w, bias=0.0, scale=1.0):
+        op("A", lambda: g.scalar.activation(out, a, fn, bias=bias, scale=scale), r, w)
+
+    def mm(out, l, rr, st, sp, r, w):
+        op("P", lambda: g.tensor.matmul(out, l, rr, st, sp), r, w)
+
+    def load(q, name, out, in_, w):
+        e = {"S": g.sync, "A": g.scalar}[q]
+        op(q, lambda: e.dma_start(out, in_), [], [w], dma="d_" + name)
+
+    def store(q, name, out, in_, r):
+        e = {"S": g.sync, "A": g.scalar}[q]
+        op(q, lambda: e.dma_start(out, in_), [r], [], dma="d_" + name)
+
+    def ms(ap, c, w):
+        op("V", lambda: g.vector.memset(ap, c), [], [w])
+
+    def diag(o, mat, mo, src, so, n, r, wb, first=True):
+        for j in range(16):
+            mm(o, T[mat][:, mo + 16 - j:mo + 144 - j], T[src][:, so + j:so + 192 * n:16], first and j == 0, j == 15, r + [mat], [wb])
+
+    B = [T["bk%d" % i] for i in range(8)]
+    SP = T.SC[:, 15:16]
+
+    load("S", "dn", T.nmi[:, 0:NP], T.nt[:, :], "nmi_n")
+    load("S", "dm", T.nmi[:, NP:2 * NP], T.mh[:, :], "nmi_m")
+    load("S", "dth", T.nmi[:, 2 * NP:3 * NP], T.th[:, :], "nmi_t")
+    load("A", "dh", T.hai[:, :], T.hands[:, :], "hai")
+    load("A", "dt", T.tri[:, :], T.trains[:, :], "tri")
+    load("A", "dx", T.X[:, 0:3072], T.x0[:, :], "X")
+    load("S", "dw", T.wti[:, :], T.wt[:, :], "wti")
+
+    op("G", lambda: g.iota(T.cwi[:, :], [[1, 16]], 128, -1), [], ["cwi"])
+    op("G", lambda: g.iota(T.smA[:, :], [[0, 16], [1, 16]], 0, 0, allow_small_or_imprecise_dtypes=True), [], ["smA"])
+    op("G", lambda: g.iota(T.iq[:, :], [[16, 12]], 0, 0, allow_small_or_imprecise_dtypes=True), [], ["iq"])
+    ms(T.R8[:, :], 1.0, "R8")
+    ms(T.smB[:, 0:16], -99.0, "smBp")
+    ms(T.X[:, 3072:CW], 0.0, "Xp")
+    ms(T.onesf[:, :], 1.0, "onesf")
+    ms(T.ones[:, :], 1.0, "ones")
+    for b in (6, 7):
+        ms(B[b][:, 192:256], 0.0, "bk%d" % b)
+    blk = [[0, 2], [-16, 8], [0, 16]]
+    blk2 = [[0, 2], [16, 8], [0, 16]]
+    op("G", lambda: g.affine_select(T.R8[:, :], T.R8[:, :], [[1, 128]], OP.is_ge, 0.0, 0, -16), ["R8"], ["R8"])
+    op("G", lambda: g.affine_select(T.R8[:, :], T.R8[:, :], [[-1, 128]], OP.is_ge, 0.0, 15, 16), ["R8"], ["R8"])
+    for nm, fill, o in (("smB", -99.0, 16), ("smC", 99.0, 0)):
+        op("G", lambda nm=nm, fill=fill, o=o: g.affine_select(T[nm][:, o:o + 256], T.smA[:, :], blk, OP.is_ge, fill, 0, 1), ["smA"], [nm])
+        op("G", lambda nm=nm, fill=fill, o=o: g.affine_select(T[nm][:, o:o + 256], T[nm][:, o:o + 256], blk2, OP.is_ge, fill, 15, -1), [nm], [nm])
+    op("G", lambda: g.iota(T.IOT[:, :], [[1, 3072]], -1536, 0, allow_small_or_imprecise_dtypes=True), [], ["IOT"])
+
+    ts(T.cwj[:, :], T.cwi[:, :], 15, OP.bitwise_and, None, None, ["cwi"], ["cwj"])
+    cp(T.cw[:, :], T.cwj[:, :], ["cwj"], ["cw"])
+    ts(T.SC[:, :], T.cw[:, :], -1.0, OP.mult, 15.0, OP.add, ["cw"], ["SC"])
+    ts(T.E0[:, :], T.cw[:, :], 0.0, OP.is_equal, None, None, ["cw"], ["E0"])
+    ts(T.bi[:, :], T.iq[:, :], SP, OP.add, None, None, ["iq", "SC"], ["bi"])
+    ts(T.cols[:, 0:1], SP, 1.0, OP.is_ge, None, None, ["SC"], ["cols"])
+    ts(T.cols[:, 1:2], SP, -1.0, OP.add, None, None, ["SC"], ["cols"])
+    ts(T.cols[:, 2:3], SP, -1.0, OP.mult, 16.0, OP.add, ["SC"], ["cols"])
+    for j, (row, v) in enumerate(((0, 1536.0), (0, -4096.0), (0, 512.0), (0, -1025.0 / 2048), (0, 1.0), (0, 2048.0), (0, 6144.0), (0, -512.0))):
+        ts(T.cols[:, 3 + j:4 + j], T.E0[:, row:row + 1], v, OP.mult, None, None, ["E0"], ["cols"])
+    ts(T.PC[:, :], T.E0[:, :], 5632.0, OP.mult, -4096.0, OP.add, ["E0"], ["PC"])
+    ts(T.WB[:, :], T.SC[:, :], -4096.0, OP.mult, 4096.0 * 16.5, OP.add, ["SC"], ["WB"])
+    ts(T.b16h[:, :], T.bi[:, :], 16.0, OP.mult, None, None, ["bi"], ["b16h"])
+    ts(T.b16i[:, :], T.bi[:, :], 16.0, OP.mult, None, None, ["bi"], ["b16i"])
+    for t in range(V):
+        ts(T.b37[:, 12 * t:12 * t + 12], T.bi[:, :], 37.0, OP.mult, float(613 * t + (CA if t else 0)), OP.add, ["bi"], ["b37"])
+
+    smb = T.smB[:, 16:144]
+    smb2 = T.smB[:, 16:272]
+    smp = T.smB[:, 0:144]
+    for t in range(V):
+        ts(T.Wr[:, 144 * t:144 * t + 144], smp, 0.0, OP.is_equal, T.E0[:, t:t + 1], OP.mult, ["smB", "smBp", "E0"], ["Wr"])
+
+    cp(T.nmf[:, :], T.nmi[:, :], ["nmi_n", "nmi_m", "nmi_t"], ["nmf"])
+    for j, b in ((1, 4), (0, 5), (2, 6)):
+        mm(B[b][:, 0:NP], T.R8[:, :], T.nmf[:, NP * j:NP * j + NP], True, True, ["R8", "nmf"], ["bk%d" % b])
+    ts(T.oyt[:, :], B[4][:, 0:NP], SP, OP.is_le, 3072.0, OP.mult, ["bk4", "SC"], ["tb"])
+    tt(T.oyb[:, :], T.oyt[:, :], T.hai[:, :], OP.max, ["tb", "hai"], ["h0f"])
+    ts(T.Hs[:, :], T.oyb[:, :], -1536.0, OP.add, None, None, ["h0f"], ["Hs"])
+    diag(B[2][:, 408:420], "Wr", 0, "Hs", 0, 1, ["Hs"], "bk2")
+    ts(T.oyh[:, :], B[5][:, 0:NP], SP, OP.is_le, 3072.0, OP.mult, ["bk5", "SC"], ["ta"])
+    tt(T.oya[:, :], T.oyh[:, :], T.tri[:, :], OP.max, ["ta", "tri"], ["t0f"])
+    cp(T.TT0[:, :], T.oya[:, :], ["t0f"], ["TT0"])
+    act(T.thr[:, :], B[6][:, 0:NP], AF.Copy, ["bk6"], ["thr"])
+
+    def S(j):
+        return T.sm[:, 12 * j:12 * j + 12]
+
+    def empties():
+        pd = B[2][:, 408:420]
+        ts(S(2), pd, EMPTY, OP.is_ge, -8192.0, OP.mult, ["bk2"], ["s2"])
+        ts(S(3), pd, 1536.0, OP.add, None, None, ["bk2"], ["s3"])
+        tt(S(0), S(3), S(2), OP.add, ["s2", "s3"], ["s0"])
+        ts(S(1), S(2), -1.0, OP.mult, -8192.0, OP.add, ["s2"], ["s1"])
+
+    empties()
+    cp(T.smi[:, 0:12], T.b37[:, 0:12], ["b37"], ["fi"])
+    ts(T.smi[:, 12:24], T.smi[:, 0:12], 2047, OP.bitwise_and, None, None, ["fi"], ["fj"])
+    tt(S(4), S(1), T.smi[:, 12:24], OP.add, ["fj", "s1"], ["s4"])
+    tt(T.cf[:, :], S(0), S(4), OP.max, ["s0", "s4"], ["cf"])
+    cp(T.cl[:, :], T.cf[:, :], ["cf"], ["cl"])
+
+    ts(T.Ib[:, :], smb, SP, OP.is_equal, None, None, ["smB", "SC"], ["Ib"])
+    ts(T.NB[:, :], smb, 0.0, OP.is_ge, -1.0, OP.mult, ["smB"], ["NB"])
+    ts(T.W2[:, :], smp, 0.0, OP.is_equal, 2.0, OP.mult, ["smB", "smBp"], ["W2"])
+    ts(T.WN[:, :], smp, 0.0, OP.is_equal, -1.0, OP.mult, ["smB", "smBp"], ["WN"])
+    ts(T.BA[:, :], smb, 0.0, OP.is_ge, None, None, ["smB"], ["BA"])
+    ts(T.I8[:, :], smb, SP, OP.is_equal, 8192.0, OP.mult, ["smB", "SC"], ["I8"])
+
+    def consts2():
+        ts(T.W256[:, :], smp, 0.0, OP.is_equal, 256.0, OP.mult, ["smB", "smBp"], ["W256"])
+        ts(T.Wk[:, :], smp, 0.0, OP.is_equal, T.cols[:, 0:1], OP.mult, ["smB", "smBp", "cols"], ["Wk"])
+        ts(T.Ih[:, :], smb2, SP, OP.is_equal, None, None, ["smB", "SC"], ["Ih"])
+        ts(T.SI[:, :], smb2, T.cols[:, 1:2], OP.is_equal, None, None, ["smB", "cols"], ["SI"])
+        tt(T.SI[:, :], T.SI[:, :], T.Ih[:, :], OP.subtract, ["SI", "Ih"], ["SI"])
+        ts(T.E15[:, :], smb2, 15.0, OP.is_equal, T.cols[:, 3:4], OP.mult, ["smB", "cols"], ["E15"])
+        ts(T.IN[:, :], smb2, SP, OP.is_equal, -1536.0, OP.mult, ["smB", "SC"], ["IN"])
+        ts(T.TUr[:, :], T.smC[:, :], SP, OP.is_lt, -4096.0, OP.mult, ["smC", "SC"], ["TUr"])
+        ts(T.TUi[:, :], T.smC[:, 0:128], SP, OP.is_le, None, None, ["smC", "SC"], ["TUi"])
+        ts(T.TU8[:, :], T.smC[:, 0:128], SP, OP.is_lt, 4096.0, OP.mult, ["smC", "SC"], ["TU8"])
+        ts(T.BH[:, :], smb2, 0.0, OP.is_ge, 8192.0, OP.mult, ["smB"], ["BH"])
+        ts(T.I8n[:, :], smb, SP, OP.is_equal, -4096.0, OP.mult, ["smB", "SC"], ["I8n"])
+        for nm, c in (("B15", 3), ("B8n", 4), ("B512", 5), ("Bh", 6), ("B1", 7), ("B4k", 8), ("B12k", 9), ("Bac", 10)):
+            ts(T[nm][:, :], smb, 0.0, OP.is_ge, T.cols[:, c:c + 1], OP.mult, ["smB", "cols"], [nm])
+        cp(T.oneh[:, :], T.ones[:, :], ["ones"], ["oneh"])
+        cp(T.cols[:, 12:13], T.wti[:, :], ["wti"], ["wtf"])
+        ts(T.Ww[:, :], smp, 0.0, OP.is_equal, T.cols[:, 12:13], OP.mult, ["smB", "smBp", "wtf"], ["Ww"])
+
+    def consts3():
+        for w in range(16):
+            ts(T.RW[:, 128 * w:128 * w + 128], smb, T.cw[:, w:w + 1], OP.is_equal, None, None, ["smB", "cw"], ["RW"])
+        ts(T.M8[:, :], T.smB[:, 16:144:16], 0.0, OP.is_ge, None, None, ["smB"], ["M8"])
+
+    def windows(t, lo, hi):
+        for c in range(lo, hi):
+            b = 6 + c % 2
+            for h in range(2):
+                o = 2 * c + h
+                w = (t + 1 - o) % 16
+                mm(B[b][:, 256 * h:256 * h + NP], T.RW[:, 128 * w:128 * w + 128], T.Tcap[:, :], True, True, ["RW", "Tcap"], ["bk%d" % b])
+            act(T.WIN[:, 512 * c:512 * c + 448], B[b][:, 0:448], AF.Copy, ["bk%d" % b], ["WIN"])
+
+    def hand_end(t):
+        act(T.Rv[:, :], T.WIN[:, :].indirect(T.ql[:, :]), AF.Copy, ["WIN", "ql"], ["Rv"])
+        tt(T.R2[:, :], T.Rv[:, :], T.wall[:, :], OP.max, ["Rv", "wall"], ["R2"])
+        tt(T.R3[:, :], T.R2[:, :], T.C1[:, :], OP.min, ["R2", "C1"], ["R3"])
+        tt(T.Hs[:, :], T.R3[:, :], T.Hp[:, :], OP.min, ["R3", "Hp"], ["Hs"])
+
+    def hand_begin(t):
+        ts(T.Hp[:, :], T.Hs[:, :], T.PC[:, t:t + 1], OP.max, None, None, ["Hs", "PC"], ["Hp"])
+        ts(T.IH[:, NP:2 * NP], T.Hp[:, :], EMPTY, OP.is_ge, None, None, ["Hp"], ["hinv"])
+
+    for t in range(V):
+        last = t == V - 1
+        tab = T["TT%d" % t]
+        tn = "TT%d" % t
+        jj = 0 if last else (2 if t == 3 else 1)
+        ro = 128 - 16 * jj
+
+        def rot(nm):
+            return T[nm][:, ro:ro + 128] if jj else T[nm][:, 0:128]
+
+        if t > 0:
+            k = op("R", None, [], [tn], dma="arr%d" % t)
+        cp(T.xc[:, :], T.X[:, :].indirect(T.cl[:, :]), ["X", "Xp", "cl"], ["xc"])
+        cp(T.XT[:, 0:1024], T.X[:, :].indirect(tab[:, 0:64]), ["X", "Xp", tn], ["XT0"])
+        for c in (1, 2):
+            act(T.XT[:, 1024 * c:1024 * c + 1024], T.X[:, :].indirect(tab[:, 64 * c:64 * c + 64]), AF.Copy, ["X", "Xp", tn], ["XT%d" % c])
+        act(T.crep[:, :], T.IOT[:, :].indirect(T.cl[:, :]), AF.Copy, ["IOT", "cl"], ["crep"])
+        ts(T.Th[:, :], tab[:, :], -1536.0, OP.add, None, None, [tn], ["Th"])
+        ts(T.IH[:, 0:NP], tab[:, :], 3072.0, OP.is_ge, None, None, [tn], ["inv"])
+        mm(B[1][:, 0:NP], T.Ib[:, :], T.xc[:, :], True, True, ["Ib", "xc"], ["bk1"])
+        mm(B[0][:, 0:NP], T.NB[:, :], T.xc[:, :], True, False, ["NB", "xc"], ["bk0"])
+        mm(B[0][:, 0:NP], T.I8[:, :], T.IH[:, 0:NP], False, False, ["I8", "inv"], ["bk0"])
+        mm(B[2][:, 0:NP], T.BA[:, :], T.IH[:, 0:NP], True, True, ["BA", "inv"], ["bk2"])
+
+        def chunk(c, lastc):
+            for s in range(16):
+                tt(T.MX[:, 1024 * c + s:1024 * c + 1024:16], B[1][:, 64 * c:64 * c + 64], T.XT[:, 1024 * c + s:1024 * c + 1024:16], OP.max,
+                   ["bk1", "XT%d" % c], ["MX%d_%d" % (c, s // 4)])
+
+        def chunkp(c, lastc):
+            for s in range(16):
+                mm(B[0][:, 64 * c:64 * c + 64], T.WN[:, 16 - s:144 - s], T.XT[:, 1024 * c + s:1024 * c + 1024:16], False, False, ["WN", "XT%d" % c], ["bk0"])
+            for s in range(16):
+                mm(B[0][:, 64 * c:64 * c + 64], T.W2[:, 16 - s:144 - s], T.MX[:, 1024 * c + s:1024 * c + 1024:16], False, lastc and s == 15,
+                   ["W2", "MX%d_%d" % (c, s // 4)], ["bk0"])
+
+        chunk(0, False)
+        chunkp(0, False)
+        if t == 0:
+            consts2()
+        if t > 0:
+            windows(t - 1, 4, 8)
+            hand_end(t - 1)
+        hand_begin(t)
+        mm(B[2][:, NP:2 * NP], T.BA[:, :], T.IH[:, NP:2 * NP], True, True, ["BA", "hinv"], ["bk2"])
+        diag(B[2][:, 384:408], "W256", 0, "IH", 0, 2, ["inv", "hinv"], "bk2")
+        if not last:
+            diag(B[2][:, 408:420], "Wr", 144 * (t + 1), "Hp", 0, 1, ["Hp"], "bk2")
+        mm(B[3][:, NP:2 * NP], rot("Ih"), T.Th[:, :], True, True, ["Ih", "Th"], ["bk3"])
+        act(T.Trot[:, :], B[3][:, NP:2 * NP], AF.Copy, ["bk3"], ["Trot"])
+        chunk(1, False)
+        chunkp(1, False)
+        act(T.wall[:, :], B[2][:, NP:2 * NP], AF.Identity, ["bk2", "WB"], ["wall"], bias=T.WB[:, t:t + 1], scale=-4096.0)
+        ts(T.ff[:, :], B[2][:, 0:NP], 0.0, OP.is_equal, None, None, ["bk2"], ["ff"])
+        ts(T.oh[:, :], B[2][:, 0:NP], 1.0, OP.max, T.cols[:, 2:3], OP.is_equal, ["bk2", "cols"], ["oh"])
+        tt(T.fT[:, :], T.ff[:, :], T.Th[:, :], OP.mult, ["ff", "Th"], ["fT"])
+        tt(T.ohc[:, :], T.oh[:, :], T.crep[:, :], OP.mult, ["oh", "crep"], ["ohc"])
+        ts(T.hoc[:, :], B[2][:, NP:2 * NP], T.SC[:, t:t + 1], OP.add, 16.0, OP.is_equal, ["bk2", "SC"], ["hoc"])
+        tt(T.x1[:, :], B[2][:, 384:396], T.bi[:, :], OP.add, ["bk2", "bi"], ["x1"])
+        tt(T.smi[:, 24:36], B[2][:, 396:408], T.x1[:, :], OP.add, ["bk2", "x1"], ["x2"])
+        ts(T.smi[:, 36:48], T.smi[:, 24:36], 4095, OP.bitwise_and, None, None, ["x2"], ["x3"])
+        cp(T.ql[:, :], T.smi[:, 36:48], ["x3"], ["ql"])
+        if not last:
+            ts(T.nd[:, :], B[2][:, 384:396], -1.0 / 256, OP.mult, 16.0, OP.add, ["bk2"], ["nd"])
+            empties()
+            tt(S(5), T.cf[:, :], S(1), OP.add, ["cf", "s1"], ["s5"])
+            ts(S(6), S(5), -8192.0, OP.add, None, None, ["s5"], ["s6"])
+        pt = B[3][:, 0:NP]
+        mm(pt, rot("Ih"), T.Th[:, :], True, False, ["Ih", "Th"], ["bk3"])
+        mm(pt, rot("SI"), T.fT[:, :], False, False, ["SI", "fT"], ["bk3"])
+        mm(pt, rot("E15"), T.ff[:, :], False, False, ["E15", "ff"], ["bk3"])
+        mm(pt, rot("IN"), T.oh[:, :], False, False, ["IN", "oh"], ["bk3"])
+        mm(pt, rot("Ih"), T.ohc[:, :], False, False, ["Ih", "ohc"], ["bk3"])
+        mm(B[6][:, 0:NP], T.B15[:, :], T.oneh[:, :], True, False, ["B15", "oneh"], ["bk6"])
+        mm(B[5][:, 0:12], T.Ih[:, 0:128], T.b16h[:, :], True, False, ["Ih", "b16h"], ["bk5"])
+        act(T.na[:, :], T.xc[:, :], AF.Copy, ["xc"], ["na"], scale=-1.0)
+        if t == 0:
+            act(T.lim[:, :], T.thr[:, :], AF.Copy, ["thr"], ["lim"])
+        else:
+            act(T.lim[:, :], T.thr[:, :], AF.Identity, ["thr", "a256"], ["lim"], bias=T.aa[:, 1:2])
+        chunk(2, True)
+        chunkp(2, True)
+
+        tt(T.ok[:, :], B[0][:, 0:NP], T.lim[:, :], OP.is_le, ["bk0", "lim"], ["ok"])
+        mm(B[4][:, 0:NP], T.TUi[:, :], T.ok[:, :], True, True, ["TUi", "ok"], ["bk4"])
+        mm(B[6][:, 0:NP], rot("TUr"), T.ok[:, :], False, True, ["TUr", "ok"], ["bk6"])
+        mm(pt, rot("BH"), T.ok[:, :], False, True, ["BH", "ok"], ["bk3"])
+        mm(B[7][:, 0:NP], T.Ib[:, :], T.xc[:, :], True, False, ["Ib", "xc"], ["bk7"])
+        mm(B[7][:, 0:NP], T.Bac[:, :], T.oneh[:, :], False, False, ["Bac", "oneh"], ["bk7"])
+        ts(T.K1[:, :], B[4][:, 0:NP], 0.5, OP.is_ge, None, None, ["bk4"], ["K1"])
+        mm(B[7][:, 0:NP], T.B512[:, :], T.K1[:, :], False, True, ["B512", "K1"], ["bk7"])
+        diag(B[5][:, 0:12], "Wk", 0, "K1", 0, 1, ["K1"], "bk5", first=False)
+        mm(B[1][:, NP:2 * NP], T.B1[:, :], T.oneh[:, :], True, False, ["B1", "oneh"], ["bk1"])
+        mm(B[1][:, NP:2 * NP], T.Bh[:, :], T.K1[:, :], False, True, ["Bh", "K1"], ["bk1"])
+        if not last:
+            diag(B[0][:, 192:204], "Wr", 0, "K1", 0, 1, ["K1"], "bk0")
+        tt(T.fst[:, :], B[6][:, 0:NP], T.Trot[:, :], OP.max, ["bk6", "Trot"], ["fst"])
+        tt(T.Tc[:, :], B[3][:, 0:NP], T.fst[:, :], OP.min, ["bk3", "fst"], ["Tc"])
+        if not last:
+            to = T["TO%d" % t]
+            nxt = T.cores[(rank + 1) % len(T.cores)]
+            ts(to[:, :], T.Tc[:, :], 1536.0, OP.add, None, None, ["Tc"], ["TO%d" % t])
+            rid, pid = topo.addr(nxt, core)
+            eng = topo.engines(core, nxt)[:8]
+            mask = 0
+            for e in eng:
+                mask |= 1 << e
+            op("G", lambda to=to, t=t, rid=rid, pid=pid, mask=mask: g.remote_dma(T["TT%d" % (t + 1)][:, :], to[:, :], T.sem["arr%d" % (t + 1)], T.sem.snd, pid, rid, mask),
+               ["TO%d" % t], [], dma="snd")
+        tt(T.ac[:, :], B[7][:, 0:NP], T.na[:, :], OP.max, ["bk7", "na"], ["ac"])
+        cp(T.kl[:, :], B[5][:, 0:12], ["bk5"], ["kl"])
+        tt(T.vv[:, :], T.XT[:, :].indirect(T.kl[:, :]), T.ac[:, :], OP.add, ["XT0", "XT1", "XT2", "kl", "ac"], ["vv"])
+        tt(T.uu[:, :], B[1][:, NP:2 * NP], T.vv[:, :], OP.mult, ["bk1", "vv"], ["uu"])
+        act(T.au[:, :], T.uu[:, :], AF.Abs, ["uu"], ["au"])
+        if not last:
+            tt(S(7), B[0][:, 192:204], T.nd[:, :], OP.mult, ["bk0", "nd"], ["s7"])
+            tt(S(8), S(7), B[5][:, 0:12], OP.subtract, ["s7", "bk5"], ["s8"])
+        ts(T.y[:, :], T.au[:, :], RND, OP.add, -RND, OP.add, ["au"], ["y"])
+        diag(B[1][:, 0:12], "Ww", 0, "y", 0, 1, ["y"], "bk1")
+        if not last:
+            op("V", lambda: g.vector.tensor_reduce(T.aa[:, 0:1], S(8), AxisListType.X, OP.add), ["s8"], ["ar"])
+            mm(B[0][:, 208:209], T.onesf[:, :], T.aa[:, 0:1], True, True, ["onesf", "ar"], ["bk0"])
+            ts(S(9), B[0][:, 192:204], -8192.0, OP.mult, None, None, ["bk0"], ["s9"])
+            tt(S(2), S(6), S(9), OP.subtract, ["s6", "s9"], ["s2"])
+            tt(S(3), S(0), S(2), OP.max, ["s0", "s2"], ["s3"])
+            tt(S(4), S(1), S(9), OP.add, ["s1", "s9"], ["s4"])
+        cp(T.zi[:, :], B[1][:, 0:12], ["bk1"], ["zi"])
+        ts(T.zj[:, :], T.zi[:, :], 15, OP.bitwise_and, None, None, ["zi"], ["zj"])
+        tt(T.zk[:, :], T.zj[:, :], T.b16i[:, :], OP.add, ["zj", "b16i"], ["zk"])
+        cp(T.zl[:, :], T.zk[:, :], ["zk"], ["zl"])
+        cp(T.X[:, :].indirect(T.zl[:, :]), T.y[:, :], ["y", "zl", "Xp"], ["X"])
+        if not last:
+            ts(T.smi[:, 0:12], T.b37[:, 12 * t + 12:12 * t + 24], B[0][:, 208:209], OP.add, None, None, ["b37", "bk0"], ["fi"])
+            ts(T.smi[:, 12:24], T.smi[:, 0:12], 2047, OP.bitwise_and, None, None, ["fi"], ["fj"])
+            tt(S(5), S(4), T.smi[:, 12:24], OP.add, ["s4", "fj"], ["s5"])
+            tt(T.cf[:, :], S(3), S(5), OP.max, ["s3", "s5"], ["cf"])
+            cp(T.cl[:, :], T.cf[:, :], ["cf"], ["cl"])
+            ts(T.ai[:, 0:1], B[0][:, 208:209], float(CA), OP.add, None, None, ["bk0"], ["ai0"])
+            ts(T.ai[:, 1:2], T.ai[:, 0:1], 255, OP.bitwise_and, None, None, ["ai0"], ["ai1"])
+            cp(T.aa[:, 1:2], T.ai[:, 1:2], ["ai1"], ["a256"])
+        if t == 0:
+            consts3()
+        mm(B[4][:, NP:2 * NP], T.B4k[:, :], T.oneh[:, :], True, False, ["B4k", "oneh"], ["bk4"])
+        mm(B[4][:, NP:2 * NP], T.TU8[:, :], T.ok[:, :], False, False, ["TU8", "ok"], ["bk4"])
+        mm(B[4][:, NP:2 * NP], T.B8n[:, :], T.K1[:, :], False, True, ["B8n", "K1"], ["bk4"])
+        mm(B[3][:, NP:2 * NP], T.B12k[:, :], T.oneh[:, :], True, False, ["B12k", "oneh"], ["bk3"])
+        mm(B[3][:, NP:2 * NP], T.I8n[:, :], T.hoc[:, :], False, False, ["I8n", "hoc"], ["bk3"])
+        mm(B[3][:, NP:2 * NP], T.B8n[:, :], T.K1[:, :], False, True, ["B8n", "K1"], ["bk3"])
+        tt(T.Tcap[:, :], B[4][:, NP:2 * NP], T.Th[:, :], OP.max, ["bk4", "Th"], ["Tcap"])
+        tt(T.C1[:, :], B[3][:, NP:2 * NP], T.crep[:, :], OP.max, ["bk3", "crep"], ["C1"])
+        windows(t, 0, 8 if last else 4)
+        if last:
+            hand_end(t)
+
+    op("S", lambda: g.sync.dma_start(T.yx[:, :], T.X[:, 0:3072]), ["X"], [], dma="d_ox")
+    ts(T.oya[:, :], T.Tc[:, :], 1536.0, OP.add, None, None, ["Tc"], ["oya"])
+    ts(T.IH[:, 0:NP], T.Tc[:, :], EMPTY, OP.is_lt, None, None, ["Tc"], ["inv"])
+    tt(T.oyt[:, :], T.oya[:, :], T.IH[:, 0:NP], OP.mult, ["oya", "inv"], ["oyt"])
+    store("S", "ot", T.yt[:, :], T.oyt[:, :], "oyt")
+    ts(T.IH[:, NP:2 * NP], T.Hs[:, :], EMPTY, OP.is_lt, None, None, ["Hs"], ["hinv"])
+    mm(B[0][0:8, 0:2 * NP], T.M8[:, :], T.IH[:, :], True, True, ["M8", "inv", "hinv"], ["bk0"])
+    ts(T.SC[:, 0:1], T.SC[:, V - 1:V], 0.0, OP.add, None, None, ["SC"], ["SCx"])
+    ts(T.Bh[:, :], smb, T.SC[:, 0:1], OP.is_equal, None, None, ["smB", "SCx"], ["Bh"])
+    mm(B[1][:, 0:NP], T.Bh[:, :], T.Hs[:, :], True, True, ["Bh", "Hs"], ["bk1"])
+    ts(T.oyb[:, :], B[1][:, 0:NP], 1536.0, OP.add, None, None, ["bk1"], ["oyb"])
+    ts(T.oya[:, :], B[1][:, 0:NP], EMPTY, OP.is_lt, None, None, ["bk1"], ["oya"])
+    tt(T.oyh[:, :], T.oya[:, :], T.oyb[:, :], OP.mult, ["oya", "oyb"], ["oyh"])
+    cp(T.omn[:, :], B[0][0:8, 0:2 * NP], ["bk0"], ["omn"])
+    store("S", "oh", T.yh[:, :], T.oyh[:, :], "oyh")
+    op("A", lambda: g.scalar.dma_start(T.yn[:, :], T.omn[:, 0:NP]), ["omn"], [], dma="d_on")
+    op("A", lambda: g.scalar.dma_start(T.ym[:, :], T.omn[:, NP:2 * NP]), ["omn"], [], dma="d_om")
+
+    emit(g, core, T, topo, ops, rank)
+
+
+def emit(g, core, T, topo, ops, rank):
+    Q = {"V": g.vector, "A": g.scalar, "P": g.tensor, "G": g, "S": g.sync}
+    sems = {"V": "qV", "A": "qA", "P": "qP", "G": "qG"}
+    seq = {}
+    for k, o in enumerate(ops):
+        seq.setdefault(o["q"], []).append(k)
+    pos = {}
+    for q in seq:
+        for i, k in enumerate(seq[q]):
+            pos[k] = i
+    know = {q: ({}, set()) for q in "VAPGS"}
+    after = {}
+    needed = set()
+    waits = {}
+    for k, o in enumerate(ops):
+        q = o["q"]
+        if q == "R":
+            after[k] = ({}, set())
+            continue
+        kn, kd = know[q]
+        wl = []
+        need = {}
+        for d in sorted(o["deps"], reverse=True):
+            od = ops[d]
+            if od["dma"]:
+                if d not in kd:
+                    wl.append(d)
+                    kd.add(d)
+                    kn2, kd2 = after[d]
+                    for a in kn2:
+                        kn[a] = max(kn.get(a, -1), kn2[a])
+                    kd |= kd2
+            else:
+                if kn.get(od["q"], -1) < pos[d]:
+                    need[od["q"]] = max(need.get(od["q"], -1), pos[d])
+        for q2 in sorted(need, key=lambda a: -seq[a][need[a]]):
+            p = need[q2]
+            if kn.get(q2, -1) >= p:
+                continue
+            d = seq[q2][p]
+            wl.append(d)
+            needed.add(d)
+            kn[q2] = p
+            kn2, kd2 = after[d]
+            for a in kn2:
+                kn[a] = max(kn.get(a, -1), kn2[a])
+            kd |= kd2
+        waits[k] = wl
+        after[k] = (dict(kn), set(kd))
+    for q in "VAPG":
+        if q in seq:
+            comp = [k for k in seq[q] if not ops[k]["dma"]]
+            if comp:
+                needed.add(comp[-1])
+    count = {}
+    cnt = {q: 0 for q in "VAPG"}
+    for k, o in enumerate(ops):
+        if k in needed:
+            cnt[o["q"]] += 1
+            count[k] = cnt[o["q"]]
+    prev = T.cores[(rank - 1) % len(T.cores)]
+    ein = len(topo.engines(prev, core)[:8])
+    nxt = T.cores[(rank + 1) % len(T.cores)]
+    eout = len(topo.engines(core, nxt)[:8])
+    nsend = 0
+    for k, o in enumerate(ops):
+        q = o["q"]
+        if q == "R":
+            continue
+        e = Q[q]
+        for d in waits[k]:
+            od = ops[d]
+            if od["dma"]:
+                e.wait_ge(T.sem[od["dma"]], ein if od["dma"][:3] == "arr" else 16)
+            else:
+                e.wait_ge(T.sem[sems[od["q"]]], count[d])
+        ins = o["f"]()
+        if o["dma"] == "snd":
+            nsend += 1
+        elif o["dma"]:
+            ins.then_inc(T.sem[o["dma"]], 16)
+        elif k in needed:
+            ins.then_inc(T.sem[sems[q]], 1)
+    for k, o in enumerate(ops):
+        if o["dma"] and o["dma"] != "snd":
+            g.wait_ge(T.sem[o["dma"]], ein if o["dma"][:3] == "arr" else 16)
+    g.wait_ge(T.sem.snd, eout * nsend)
+    for q in "VAPG":
+        if cnt[q]:
+            g.wait_ge(T.sem[sems[q]], cnt[q])

@@ -1,6 +1,4 @@
-from concourse.bass import DstId, RemoteDMATransfer
-from concourse.mybir import dt, AluOpType, AxisListType, ActivationFunctionType
-import math
+from concourse.mybir import AluOpType, AxisListType, ActivationFunctionType
 
 OP = AluOpType
 AF = ActivationFunctionType
@@ -8,7 +6,7 @@ V = 6
 NP = 192
 CW = 3088
 EMPTY = 1536.0
-PARTS = ("MX", "cols", "Wr", "b", "RW", "WIN")
+PARTS = ("MX", "cols", "Wr", "b", "RW", "WIN", "MB")
 CA = 8 * 16 * (191 * 192 // 2)
 RND = 8388608.0
 
@@ -30,30 +28,27 @@ SCRATCH = {
     "onesf": ("sbuf", [128, 128], "float32"), "ones": ("sbuf", [128, NP], "bfloat16"), "oneh": ("sbuf", [128, NP], "float16"),
     "Ib": ("sbuf", [128, 128], "bfloat16"), "NB": ("sbuf", [128, 128], "bfloat16"),
     "W2": ("sbuf", [128, 144], "bfloat16"), "WN": ("sbuf", [128, 144], "bfloat16"), "Ww": ("sbuf", [128, 144], "bfloat16"),
-    "Wk": ("sbuf", [128, 144], "float16"), "Wr": ("sbuf", [128, 144 * V], "float16"), "W256": ("sbuf", [128, 144], "float16"),
+    "Wk": ("sbuf", [128, 144], "float16"), "W0": ("sbuf", [128, 144], "float16"), "W256": ("sbuf", [128, 144], "float16"),
     "Ih": ("sbuf", [128, 256], "float16"), "SI": ("sbuf", [128, 256], "float16"), "E15": ("sbuf", [128, 256], "float16"),
     "IN": ("sbuf", [128, 256], "float16"), "TUr": ("sbuf", [128, 256], "float16"), "BA": ("sbuf", [128, 128], "float16"),
     "BH": ("sbuf", [128, 256], "float16"), "TUi": ("sbuf", [128, 128], "float16"), "TU8": ("sbuf", [128, 128], "float16"),
-    "I8": ("sbuf", [128, 128], "float16"), "I8n": ("sbuf", [128, 128], "float16"), "B15": ("sbuf", [128, 128], "float16"),
-    "B8n": ("sbuf", [128, 128], "float16"), "B512": ("sbuf", [128, 128], "float16"), "Bh": ("sbuf", [128, 128], "float16"),
-    "Bac": ("sbuf", [128, 128], "float16"), "B1": ("sbuf", [128, 128], "float16"), "B4k": ("sbuf", [128, 128], "float16"),
-    "B12k": ("sbuf", [128, 128], "float16"), "M8": ("sbuf", [128, 8], "float16"),
+    "I8": ("sbuf", [128, 128], "float16"), "I8n": ("sbuf", [128, 128], "float16"), "MB": ("sbuf", [128, 8 * 128], "float16"),
+    "M8": ("sbuf", [128, 8], "float16"), "UR": ("sbuf", [128, 128], "float16"),
     "thr": ("sbuf", [128, NP], "float32"), "lim": ("sbuf", [128, NP], "float32"),
-    "Th": ("sbuf", [128, NP], "float16"), "IH": ("sbuf", [128, 2 * NP], "float16"), "Hs": ("sbuf", [128, NP], "float16"),
+    "Th": ("sbuf", [128, NP], "float16"), "IH": ("sbuf", [128, 3 * NP], "float16"), "Hs": ("sbuf", [128, NP], "float16"),
     "Hp": ("sbuf", [128, NP], "float16"), "ff": ("sbuf", [128, NP], "float16"), "oh": ("sbuf", [128, NP], "float16"),
     "fT": ("sbuf", [128, NP], "float16"), "ohc": ("sbuf", [128, NP], "float16"), "crep": ("sbuf", [128, NP], "float32"),
     "Trot": ("sbuf", [128, NP], "float32"), "xc": ("sbuf", [128, NP], "bfloat16"), "na": ("sbuf", [128, NP], "float32"),
     "ok": ("sbuf", [128, NP], "float16"), "K1": ("sbuf", [128, NP], "float16"), "fst": ("sbuf", [128, NP], "float16"),
     "Tc": ("sbuf", [128, NP], "float16"), "ac": ("sbuf", [128, NP], "float32"), "vv": ("sbuf", [128, NP], "float32"),
     "uu": ("sbuf", [128, NP], "float32"), "au": ("sbuf", [128, NP], "float32"), "y": ("sbuf", [128, NP], "bfloat16"),
-    "Tcap": ("sbuf", [128, NP], "float16"), "hoc": ("sbuf", [128, NP], "float16"), "wall": ("sbuf", [128, NP], "float32"),
+    "Tcap": ("sbuf", [128, NP], "float16"), "hoc": ("sbuf", [128, NP], "float16"),
     "C1": ("sbuf", [128, NP], "float32"), "Rv": ("sbuf", [128, NP], "float32"), "R2": ("sbuf", [128, NP], "float32"),
-    "R3": ("sbuf", [128, NP], "float32"),
     "cf": ("sbuf", [128, 12], "float32"), "cl": ("sbuf", [128, 12], "uint16"), "kl": ("sbuf", [128, 12], "uint16"),
     "zl": ("sbuf", [128, 12], "uint16"), "ql": ("sbuf", [128, 12], "uint16"),
     "zi": ("sbuf", [128, 12], "int32"), "zj": ("sbuf", [128, 12], "int32"), "zk": ("sbuf", [128, 12], "int32"),
-    "x1": ("sbuf", [128, 12], "float32"),
-    "nd": ("sbuf", [128, 12], "float32"), "sm": ("sbuf", [128, 12 * 10], "float32"), "smi": ("sbuf", [128, 12 * 4], "int32"),
+    "x1": ("sbuf", [128, 12], "float32"), "nd": ("sbuf", [128, 12], "float32"),
+    "sm": ("sbuf", [128, 12 * 10], "float32"), "smi": ("sbuf", [128, 12 * 4], "int32"),
     "aa": ("sbuf", [128, 4], "float32"), "ai": ("sbuf", [128, 2], "int32"),
     "oyh": ("sbuf", [128, NP], "float32"), "oyt": ("sbuf", [128, NP], "float32"), "oya": ("sbuf", [128, NP], "float32"),
     "oyb": ("sbuf", [128, NP], "float32"), "omn": ("sbuf", [8, 2 * NP], "float32"),
@@ -67,6 +62,10 @@ for _i in range(V - 1):
 
 DMAS = ["dx", "dt", "dh", "dn", "dm", "dth", "dw", "ox", "oh", "ot", "om", "on"]
 SEMAPHORES = ["qV", "qA", "qP", "qG", "snd"] + ["arr%d" % i for i in range(1, V)] + ["d_" + n for n in DMAS]
+
+
+def send_engines(topo, src, dst):
+    return topo.engines(src, dst)[:8]
 
 
 def rank_program(g, core, T, topo):
@@ -102,10 +101,8 @@ def rank_program(g, core, T, topo):
                     if q2 != q:
                         deps.add(a[q2])
                 a[q] = k
-        ops.append({"q": q, "f": f, "deps": deps, "dma": dma, "inc": None})
+        ops.append({"q": q, "f": f, "deps": deps, "dma": dma})
         return k
-
-    Q = {"V": g.vector, "A": g.scalar, "P": g.tensor, "G": g, "S": g.sync}
 
     def ts(out, in0, s1, o1, s2, o2, r, w):
         if o2 is None:
@@ -125,35 +122,38 @@ def rank_program(g, core, T, topo):
     def mm(out, l, rr, st, sp, r, w):
         op("P", lambda: g.tensor.matmul(out, l, rr, st, sp), r, w)
 
-    def load(q, name, out, in_, w):
+    def dma(q, name, out, in_, r, w):
         e = {"S": g.sync, "A": g.scalar}[q]
-        op(q, lambda: e.dma_start(out, in_), [], [w], dma="d_" + name)
-
-    def store(q, name, out, in_, r):
-        e = {"S": g.sync, "A": g.scalar}[q]
-        op(q, lambda: e.dma_start(out, in_), [r], [], dma="d_" + name)
+        op(q, lambda: e.dma_start(out, in_), r, w, dma="d_" + name)
 
     def ms(ap, c, w):
         op("V", lambda: g.vector.memset(ap, c), [], [w])
 
-    def diag(o, mat, mo, src, so, n, r, wb, first=True):
+    def MB(j):
+        return T.MB[:, 128 * j:128 * j + 128]
+
+    def S(j):
+        return T.sm[:, 12 * j:12 * j + 12]
+
+    def diag(o, mat, src, so, n, r, wb, first=True):
         for j in range(16):
-            mm(o, T[mat][:, mo + 16 - j:mo + 144 - j], T[src][:, so + j:so + 192 * n:16], first and j == 0, j == 15, r + [mat], [wb])
+            mm(o, T[mat][:, 16 - j:144 - j], T[src][:, so + j:so + NP * n:16], first and j == 0, j == 15, r + [mat], [wb])
 
     B = [T["bk%d" % i] for i in range(8)]
     SP = T.SC[:, 15:16]
 
-    load("S", "dn", T.nmi[:, 0:NP], T.nt[:, :], "nmi_n")
-    load("S", "dm", T.nmi[:, NP:2 * NP], T.mh[:, :], "nmi_m")
-    load("S", "dth", T.nmi[:, 2 * NP:3 * NP], T.th[:, :], "nmi_t")
-    load("A", "dh", T.hai[:, :], T.hands[:, :], "hai")
-    load("A", "dt", T.tri[:, :], T.trains[:, :], "tri")
-    load("A", "dx", T.X[:, 0:3072], T.x0[:, :], "X")
-    load("S", "dw", T.wti[:, :], T.wt[:, :], "wti")
+    dma("S", "dm", T.nmi[:, NP:2 * NP], T.mh[:, :], [], ["nmi_m"])
+    dma("A", "dh", T.hai[:, :], T.hands[:, :], [], ["hai"])
+    dma("S", "dn", T.nmi[:, 0:NP], T.nt[:, :], [], ["nmi_n"])
+    dma("A", "dx", T.X[:, 0:3072], T.x0[:, :], [], ["X"])
+    dma("S", "dt", T.tri[:, :], T.trains[:, :], [], ["tri"])
+    dma("S", "dth", T.nmi[:, 2 * NP:3 * NP], T.th[:, :], [], ["nmi_t"])
+    dma("S", "dw", T.wti[:, :], T.wt[:, :], [], ["wti"])
 
+    blk = [[0, 2], [-16, 8], [0, 16]]
+    blk2 = [[0, 2], [16, 8], [0, 16]]
     op("G", lambda: g.iota(T.cwi[:, :], [[1, 16]], 128, -1), [], ["cwi"])
     op("G", lambda: g.iota(T.smA[:, :], [[0, 16], [1, 16]], 0, 0, allow_small_or_imprecise_dtypes=True), [], ["smA"])
-    op("G", lambda: g.iota(T.iq[:, :], [[16, 12]], 0, 0, allow_small_or_imprecise_dtypes=True), [], ["iq"])
     ms(T.R8[:, :], 1.0, "R8")
     ms(T.smB[:, 0:16], -99.0, "smBp")
     ms(T.X[:, 3072:CW], 0.0, "Xp")
@@ -161,131 +161,155 @@ def rank_program(g, core, T, topo):
     ms(T.ones[:, :], 1.0, "ones")
     for b in (6, 7):
         ms(B[b][:, 192:256], 0.0, "bk%d" % b)
-    blk = [[0, 2], [-16, 8], [0, 16]]
-    blk2 = [[0, 2], [16, 8], [0, 16]]
+
+    def blocks(nm, fill, o):
+        op("G", lambda: g.affine_select(T[nm][:, o:o + 256], T.smA[:, :], blk, OP.is_ge, fill, 0, 1), ["smA"], [nm])
+        op("G", lambda: g.affine_select(T[nm][:, o:o + 256], T[nm][:, o:o + 256], blk2, OP.is_ge, fill, 15, -1), [nm], [nm])
+
+    blocks("smB", -99.0, 16)
     op("G", lambda: g.affine_select(T.R8[:, :], T.R8[:, :], [[1, 128]], OP.is_ge, 0.0, 0, -16), ["R8"], ["R8"])
     op("G", lambda: g.affine_select(T.R8[:, :], T.R8[:, :], [[-1, 128]], OP.is_ge, 0.0, 15, 16), ["R8"], ["R8"])
-    for nm, fill, o in (("smB", -99.0, 16), ("smC", 99.0, 0)):
-        op("G", lambda nm=nm, fill=fill, o=o: g.affine_select(T[nm][:, o:o + 256], T.smA[:, :], blk, OP.is_ge, fill, 0, 1), ["smA"], [nm])
-        op("G", lambda nm=nm, fill=fill, o=o: g.affine_select(T[nm][:, o:o + 256], T[nm][:, o:o + 256], blk2, OP.is_ge, fill, 15, -1), [nm], [nm])
+    op("G", lambda: g.iota(T.iq[:, :], [[16, 12]], 0, 0, allow_small_or_imprecise_dtypes=True), [], ["iq"])
+    blocks("smC", 99.0, 0)
     op("G", lambda: g.iota(T.IOT[:, :], [[1, 3072]], -1536, 0, allow_small_or_imprecise_dtypes=True), [], ["IOT"])
-
-    ts(T.cwj[:, :], T.cwi[:, :], 15, OP.bitwise_and, None, None, ["cwi"], ["cwj"])
-    cp(T.cw[:, :], T.cwj[:, :], ["cwj"], ["cw"])
-    ts(T.SC[:, :], T.cw[:, :], -1.0, OP.mult, 15.0, OP.add, ["cw"], ["SC"])
-    ts(T.E0[:, :], T.cw[:, :], 0.0, OP.is_equal, None, None, ["cw"], ["E0"])
-    ts(T.bi[:, :], T.iq[:, :], SP, OP.add, None, None, ["iq", "SC"], ["bi"])
-    ts(T.cols[:, 0:1], SP, 1.0, OP.is_ge, None, None, ["SC"], ["cols"])
-    ts(T.cols[:, 1:2], SP, -1.0, OP.add, None, None, ["SC"], ["cols"])
-    ts(T.cols[:, 2:3], SP, -1.0, OP.mult, 16.0, OP.add, ["SC"], ["cols"])
-    for j, (row, v) in enumerate(((0, 1536.0), (0, -4096.0), (0, 512.0), (0, -1025.0 / 2048), (0, 1.0), (0, 2048.0), (0, 6144.0), (0, -512.0))):
-        ts(T.cols[:, 3 + j:4 + j], T.E0[:, row:row + 1], v, OP.mult, None, None, ["E0"], ["cols"])
-    ts(T.PC[:, :], T.E0[:, :], 5632.0, OP.mult, -4096.0, OP.add, ["E0"], ["PC"])
-    ts(T.WB[:, :], T.SC[:, :], -4096.0, OP.mult, 4096.0 * 16.5, OP.add, ["SC"], ["WB"])
-    ts(T.b16h[:, :], T.bi[:, :], 16.0, OP.mult, None, None, ["bi"], ["b16h"])
-    ts(T.b16i[:, :], T.bi[:, :], 16.0, OP.mult, None, None, ["bi"], ["b16i"])
-    for t in range(V):
-        ts(T.b37[:, 12 * t:12 * t + 12], T.bi[:, :], 37.0, OP.mult, float(613 * t + (CA if t else 0)), OP.add, ["bi"], ["b37"])
 
     smb = T.smB[:, 16:144]
     smb2 = T.smB[:, 16:272]
     smp = T.smB[:, 0:144]
-    for t in range(V):
-        ts(T.Wr[:, 144 * t:144 * t + 144], smp, 0.0, OP.is_equal, T.E0[:, t:t + 1], OP.mult, ["smB", "smBp", "E0"], ["Wr"])
+    ts(T.cwj[:, :], T.cwi[:, :], 15, OP.bitwise_and, None, None, ["cwi"], ["cwj"])
+    cp(T.cw[:, :], T.cwj[:, :], ["cwj"], ["cw"])
+    ts(T.SC[:, :], T.cw[:, :], -1.0, OP.mult, 15.0, OP.add, ["cw"], ["SC"])
+    ts(T.E0[:, :], T.cw[:, :], 0.0, OP.is_equal, None, None, ["cw"], ["E0"])
+    ts(T.cols[:, 0:1], SP, 1.0, OP.is_ge, None, None, ["SC"], ["cols"])
+    ts(T.cols[:, 1:2], SP, -1.0, OP.add, None, None, ["SC"], ["cols"])
+    ts(T.cols[:, 2:3], SP, -1.0, OP.mult, 16.0, OP.add, ["SC"], ["cols"])
+    row0 = (1536.0, -4096.0, 512.0, -1025.0 / 2048, 1.0, 2048.0, 6144.0, -512.0)
+    for j, v in enumerate(row0):
+        ts(T.cols[:, 3 + j:4 + j], T.E0[:, 0:1], v, OP.mult, None, None, ["E0"], ["cols"])
+    ts(T.PC[:, :], T.E0[:, :], 5632.0, OP.mult, -4096.0, OP.add, ["E0"], ["PC"])
+    ts(T.WB[:, :], T.SC[:, :], -4096.0, OP.mult, 4096.0 * 16.5, OP.add, ["SC"], ["WB"])
+    ts(T.W0[:, :], smp, 0.0, OP.is_equal, T.E0[:, 0:1], OP.mult, ["smB", "smBp", "E0"], ["W0"])
 
-    cp(T.nmf[:, :], T.nmi[:, :], ["nmi_n", "nmi_m", "nmi_t"], ["nmf"])
-    for j, b in ((1, 4), (0, 5), (2, 6)):
-        mm(B[b][:, 0:NP], T.R8[:, :], T.nmf[:, NP * j:NP * j + NP], True, True, ["R8", "nmf"], ["bk%d" % b])
+    def spread(j, nm, b):
+        cp(T.nmf[:, NP * j:NP * j + NP], T.nmi[:, NP * j:NP * j + NP], [nm], [nm + "f"])
+        mm(B[b][:, 0:NP], T.R8[:, :], T.nmf[:, NP * j:NP * j + NP], True, True, ["R8", nm + "f"], ["bk%d" % b])
+
+    spread(1, "nmi_m", 4)
+    ts(T.bi[:, :], T.iq[:, :], SP, OP.add, None, None, ["iq", "SC"], ["bi"])
+    for t in range(V):
+        ts(T.b37[:, 12 * t:12 * t + 12], T.bi[:, :], 37.0, OP.mult, float(613 * t + (CA if t else 0)), OP.add, ["bi"], ["b37"])
     ts(T.oyt[:, :], B[4][:, 0:NP], SP, OP.is_le, 3072.0, OP.mult, ["bk4", "SC"], ["tb"])
     tt(T.oyb[:, :], T.oyt[:, :], T.hai[:, :], OP.max, ["tb", "hai"], ["h0f"])
     ts(T.Hs[:, :], T.oyb[:, :], -1536.0, OP.add, None, None, ["h0f"], ["Hs"])
-    diag(B[2][:, 408:420], "Wr", 0, "Hs", 0, 1, ["Hs"], "bk2")
+    diag(B[2][:, 408:420], "W0", "Hs", 0, 1, ["Hs"], "bk2")
+    spread(0, "nmi_n", 5)
     ts(T.oyh[:, :], B[5][:, 0:NP], SP, OP.is_le, 3072.0, OP.mult, ["bk5", "SC"], ["ta"])
     tt(T.oya[:, :], T.oyh[:, :], T.tri[:, :], OP.max, ["ta", "tri"], ["t0f"])
     cp(T.TT0[:, :], T.oya[:, :], ["t0f"], ["TT0"])
-    act(T.thr[:, :], B[6][:, 0:NP], AF.Copy, ["bk6"], ["thr"])
 
-    def S(j):
-        return T.sm[:, 12 * j:12 * j + 12]
-
-    def empties():
+    def empties(scale):
         pd = B[2][:, 408:420]
-        ts(S(2), pd, EMPTY, OP.is_ge, -8192.0, OP.mult, ["bk2"], ["s2"])
-        ts(S(3), pd, 1536.0, OP.add, None, None, ["bk2"], ["s3"])
-        tt(S(0), S(3), S(2), OP.add, ["s2", "s3"], ["s0"])
+        ts(S(2), pd, EMPTY * scale, OP.is_ge, -8192.0, OP.mult, ["bk2"], ["s2"])
+        ts(S(3), pd, 1.0 / scale, OP.mult, 1536.0, OP.add, ["bk2"], ["s3"])
         ts(S(1), S(2), -1.0, OP.mult, -8192.0, OP.add, ["s2"], ["s1"])
+        tt(S(0), S(3), S(2), OP.add, ["s2", "s3"], ["s0"])
 
-    empties()
+    empties(1.0)
     cp(T.smi[:, 0:12], T.b37[:, 0:12], ["b37"], ["fi"])
     ts(T.smi[:, 12:24], T.smi[:, 0:12], 2047, OP.bitwise_and, None, None, ["fi"], ["fj"])
     tt(S(4), S(1), T.smi[:, 12:24], OP.add, ["fj", "s1"], ["s4"])
     tt(T.cf[:, :], S(0), S(4), OP.max, ["s0", "s4"], ["cf"])
     cp(T.cl[:, :], T.cf[:, :], ["cf"], ["cl"])
 
-    ts(T.Ib[:, :], smb, SP, OP.is_equal, None, None, ["smB", "SC"], ["Ib"])
-    ts(T.NB[:, :], smb, 0.0, OP.is_ge, -1.0, OP.mult, ["smB"], ["NB"])
-    ts(T.W2[:, :], smp, 0.0, OP.is_equal, 2.0, OP.mult, ["smB", "smBp"], ["W2"])
-    ts(T.WN[:, :], smp, 0.0, OP.is_equal, -1.0, OP.mult, ["smB", "smBp"], ["WN"])
-    ts(T.BA[:, :], smb, 0.0, OP.is_ge, None, None, ["smB"], ["BA"])
-    ts(T.I8[:, :], smb, SP, OP.is_equal, 8192.0, OP.mult, ["smB", "SC"], ["I8"])
-
-    def consts2():
-        ts(T.W256[:, :], smp, 0.0, OP.is_equal, 256.0, OP.mult, ["smB", "smBp"], ["W256"])
-        ts(T.Wk[:, :], smp, 0.0, OP.is_equal, T.cols[:, 0:1], OP.mult, ["smB", "smBp", "cols"], ["Wk"])
+    def matrices():
+        ts(T.Ib[:, :], smb, SP, OP.is_equal, None, None, ["smB", "SC"], ["Ib"])
+        ts(T.NB[:, :], smb, 0.0, OP.is_ge, -1.0, OP.mult, ["smB"], ["NB"])
+        ts(T.W2[:, :], smp, 0.0, OP.is_equal, 2.0, OP.mult, ["smB", "smBp"], ["W2"])
+        ts(T.WN[:, :], smp, 0.0, OP.is_equal, -1.0, OP.mult, ["smB", "smBp"], ["WN"])
+        ts(T.BA[:, :], smb, 0.0, OP.is_ge, None, None, ["smB"], ["BA"])
+        ts(T.I8[:, :], smb, SP, OP.is_equal, 8192.0, OP.mult, ["smB", "SC"], ["I8"])
         ts(T.Ih[:, :], smb2, SP, OP.is_equal, None, None, ["smB", "SC"], ["Ih"])
         ts(T.SI[:, :], smb2, T.cols[:, 1:2], OP.is_equal, None, None, ["smB", "cols"], ["SI"])
-        tt(T.SI[:, :], T.SI[:, :], T.Ih[:, :], OP.subtract, ["SI", "Ih"], ["SI"])
         ts(T.E15[:, :], smb2, 15.0, OP.is_equal, T.cols[:, 3:4], OP.mult, ["smB", "cols"], ["E15"])
+        tt(T.SI[:, :], T.SI[:, :], T.Ih[:, :], OP.subtract, ["SI", "Ih"], ["SI"])
         ts(T.IN[:, :], smb2, SP, OP.is_equal, -1536.0, OP.mult, ["smB", "SC"], ["IN"])
         ts(T.TUr[:, :], T.smC[:, :], SP, OP.is_lt, -4096.0, OP.mult, ["smC", "SC"], ["TUr"])
         ts(T.TUi[:, :], T.smC[:, 0:128], SP, OP.is_le, None, None, ["smC", "SC"], ["TUi"])
         ts(T.TU8[:, :], T.smC[:, 0:128], SP, OP.is_lt, 4096.0, OP.mult, ["smC", "SC"], ["TU8"])
         ts(T.BH[:, :], smb2, 0.0, OP.is_ge, 8192.0, OP.mult, ["smB"], ["BH"])
-        ts(T.I8n[:, :], smb, SP, OP.is_equal, -4096.0, OP.mult, ["smB", "SC"], ["I8n"])
-        for nm, c in (("B15", 3), ("B8n", 4), ("B512", 5), ("Bh", 6), ("B1", 7), ("B4k", 8), ("B12k", 9), ("Bac", 10)):
-            ts(T[nm][:, :], smb, 0.0, OP.is_ge, T.cols[:, c:c + 1], OP.mult, ["smB", "cols"], [nm])
+        for j in range(len(row0)):
+            ts(MB(j), smb, 0.0, OP.is_ge, T.cols[:, 3 + j:4 + j], OP.mult, ["smB", "cols"], ["MB"])
+        ts(T.b16h[:, :], T.bi[:, :], 16.0, OP.mult, None, None, ["bi"], ["b16h"])
+        ts(T.Wk[:, :], smp, 0.0, OP.is_equal, T.cols[:, 0:1], OP.mult, ["smB", "smBp", "cols"], ["Wk"])
+        ts(T.W256[:, :], smp, 0.0, OP.is_equal, 256.0, OP.mult, ["smB", "smBp"], ["W256"])
         cp(T.oneh[:, :], T.ones[:, :], ["ones"], ["oneh"])
+
+    def matrices2():
         cp(T.cols[:, 12:13], T.wti[:, :], ["wti"], ["wtf"])
+        ts(T.b16i[:, :], T.bi[:, :], 16.0, OP.mult, None, None, ["bi"], ["b16i"])
+        ts(T.I8n[:, :], smb, SP, OP.is_equal, -4096.0, OP.mult, ["smB", "SC"], ["I8n"])
         ts(T.Ww[:, :], smp, 0.0, OP.is_equal, T.cols[:, 12:13], OP.mult, ["smB", "smBp", "wtf"], ["Ww"])
 
-    def consts3():
+    def matrices3():
         for w in range(16):
             ts(T.RW[:, 128 * w:128 * w + 128], smb, T.cw[:, w:w + 1], OP.is_equal, None, None, ["smB", "cw"], ["RW"])
         ts(T.M8[:, :], T.smB[:, 16:144:16], 0.0, OP.is_ge, None, None, ["smB"], ["M8"])
+        ts(T.UR[:, :], smb, T.SC[:, V - 1:V], OP.is_equal, None, None, ["smB", "SC"], ["UR"])
 
-    def windows(t, lo, hi):
-        for c in range(lo, hi):
-            b = 6 + c % 2
-            for h in range(2):
-                o = 2 * c + h
-                w = (t + 1 - o) % 16
-                mm(B[b][:, 256 * h:256 * h + NP], T.RW[:, 128 * w:128 * w + 128], T.Tcap[:, :], True, True, ["RW", "Tcap"], ["bk%d" % b])
-            act(T.WIN[:, 512 * c:512 * c + 448], B[b][:, 0:448], AF.Copy, ["bk%d" % b], ["WIN"])
+    matrices()
+    spread(2, "nmi_t", 6)
+    act(T.thr[:, :], B[6][:, 0:NP], AF.Copy, ["bk6"], ["thr"])
+    matrices2()
 
-    def hand_end(t):
+    def windows(t, c):
+        b = 6 + c % 2
+        for h in range(2):
+            o = 2 * c + h
+            w = (t + 1 - o) % 16
+            mm(B[b][:, 256 * h:256 * h + NP], T.RW[:, 128 * w:128 * w + 128], T.Tcap[:, :], True, True, ["RW", "Tcap"], ["bk%d" % b])
+        act(T.WIN[:, 512 * c:512 * c + 448], B[b][:, 0:448], AF.Copy, ["bk%d" % b], ["WIN"])
+
+    def turned():
         act(T.Rv[:, :], T.WIN[:, :].indirect(T.ql[:, :]), AF.Copy, ["WIN", "ql"], ["Rv"])
-        tt(T.R2[:, :], T.Rv[:, :], T.wall[:, :], OP.max, ["Rv", "wall"], ["R2"])
-        tt(T.R3[:, :], T.R2[:, :], T.C1[:, :], OP.min, ["R2", "C1"], ["R3"])
-        tt(T.Hs[:, :], T.R3[:, :], T.Hp[:, :], OP.min, ["R3", "Hp"], ["Hs"])
+
+    def hand_end():
+        tt(T.R2[:, :], B[5][:, 0:NP], T.Rv[:, :], OP.max, ["Rv", "bk5", "wall"], ["R2"])
+        tt(T.Hs[:, :], B[5][:, NP:2 * NP], T.R2[:, :], OP.min, ["R2", "bk5", "R3p"], ["Hs"])
 
     def hand_begin(t):
         ts(T.Hp[:, :], T.Hs[:, :], T.PC[:, t:t + 1], OP.max, None, None, ["Hs", "PC"], ["Hp"])
         ts(T.IH[:, NP:2 * NP], T.Hp[:, :], EMPTY, OP.is_ge, None, None, ["Hp"], ["hinv"])
+        if t < V - 1:
+            ts(T.IH[:, 2 * NP:3 * NP], T.Hp[:, :], T.E0[:, t + 1:t + 2], OP.mult, None, None, ["Hp", "E0"], ["hfr"])
 
     for t in range(V):
         last = t == V - 1
-        tab = T["TT%d" % t]
         tn = "TT%d" % t
+        tab = T[tn]
         jj = 0 if last else (2 if t == 3 else 1)
         ro = 128 - 16 * jj
 
         def rot(nm):
             return T[nm][:, ro:ro + 128] if jj else T[nm][:, 0:128]
 
+        def chunk(c):
+            for s in range(16):
+                tt(T.MX[:, 1024 * c + s:1024 * c + 1024:16], B[1][:, 64 * c:64 * c + 64], T.XT[:, 1024 * c + s:1024 * c + 1024:16], OP.max,
+                   ["bk1", "XT%d" % c], ["MX%d_%d" % (c, s // 4)])
+
+        def sumx(c):
+            for s in range(16):
+                mm(B[0][:, 64 * c:64 * c + 64], T.WN[:, 16 - s:144 - s], T.XT[:, 1024 * c + s:1024 * c + 1024:16], False, False, ["WN", "XT%d" % c], ["bk0"])
+
+        def summ(c):
+            for s in range(16):
+                mm(B[0][:, 64 * c:64 * c + 64], T.W2[:, 16 - s:144 - s], T.MX[:, 1024 * c + s:1024 * c + 1024:16], False, c == 2 and s == 15,
+                   ["W2", "MX%d_%d" % (c, s // 4)], ["bk0"])
+
         if t > 0:
-            k = op("R", None, [], [tn], dma="arr%d" % t)
-        cp(T.xc[:, :], T.X[:, :].indirect(T.cl[:, :]), ["X", "Xp", "cl"], ["xc"])
+            op("R", None, [], [tn], dma="arr%d" % t)
         cp(T.XT[:, 0:1024], T.X[:, :].indirect(tab[:, 0:64]), ["X", "Xp", tn], ["XT0"])
+        act(T.xc[:, :], T.X[:, :].indirect(T.cl[:, :]), AF.Copy, ["X", "Xp", "cl"], ["xc"])
         for c in (1, 2):
             act(T.XT[:, 1024 * c:1024 * c + 1024], T.X[:, :].indirect(tab[:, 64 * c:64 * c + 64]), AF.Copy, ["X", "Xp", tn], ["XT%d" % c])
         act(T.crep[:, :], T.IOT[:, :].indirect(T.cl[:, :]), AF.Copy, ["IOT", "cl"], ["crep"])
@@ -295,154 +319,143 @@ def rank_program(g, core, T, topo):
         mm(B[0][:, 0:NP], T.NB[:, :], T.xc[:, :], True, False, ["NB", "xc"], ["bk0"])
         mm(B[0][:, 0:NP], T.I8[:, :], T.IH[:, 0:NP], False, False, ["I8", "inv"], ["bk0"])
         mm(B[2][:, 0:NP], T.BA[:, :], T.IH[:, 0:NP], True, True, ["BA", "inv"], ["bk2"])
-
-        def chunk(c, lastc):
-            for s in range(16):
-                tt(T.MX[:, 1024 * c + s:1024 * c + 1024:16], B[1][:, 64 * c:64 * c + 64], T.XT[:, 1024 * c + s:1024 * c + 1024:16], OP.max,
-                   ["bk1", "XT%d" % c], ["MX%d_%d" % (c, s // 4)])
-
-        def chunkp(c, lastc):
-            for s in range(16):
-                mm(B[0][:, 64 * c:64 * c + 64], T.WN[:, 16 - s:144 - s], T.XT[:, 1024 * c + s:1024 * c + 1024:16], False, False, ["WN", "XT%d" % c], ["bk0"])
-            for s in range(16):
-                mm(B[0][:, 64 * c:64 * c + 64], T.W2[:, 16 - s:144 - s], T.MX[:, 1024 * c + s:1024 * c + 1024:16], False, lastc and s == 15,
-                   ["W2", "MX%d_%d" % (c, s // 4)], ["bk0"])
-
-        chunk(0, False)
-        chunkp(0, False)
-        if t == 0:
-            consts2()
-        if t > 0:
-            windows(t - 1, 4, 8)
-            hand_end(t - 1)
-        hand_begin(t)
-        mm(B[2][:, NP:2 * NP], T.BA[:, :], T.IH[:, NP:2 * NP], True, True, ["BA", "hinv"], ["bk2"])
-        diag(B[2][:, 384:408], "W256", 0, "IH", 0, 2, ["inv", "hinv"], "bk2")
-        if not last:
-            diag(B[2][:, 408:420], "Wr", 144 * (t + 1), "Hp", 0, 1, ["Hp"], "bk2")
+        sumx(0)
         mm(B[3][:, NP:2 * NP], rot("Ih"), T.Th[:, :], True, True, ["Ih", "Th"], ["bk3"])
         act(T.Trot[:, :], B[3][:, NP:2 * NP], AF.Copy, ["bk3"], ["Trot"])
-        chunk(1, False)
-        chunkp(1, False)
-        act(T.wall[:, :], B[2][:, NP:2 * NP], AF.Identity, ["bk2", "WB"], ["wall"], bias=T.WB[:, t:t + 1], scale=-4096.0)
+        act(T.na[:, :], T.xc[:, :], AF.Copy, ["xc"], ["na"], scale=-1.0)
+        if t == 0:
+            act(T.lim[:, :], T.thr[:, :], AF.Copy, ["thr"], ["lim"])
+        else:
+            act(T.lim[:, :], T.thr[:, :], AF.Identity, ["thr", "a256"], ["lim"], bias=T.aa[:, 1:2])
+        chunk(0)
+        summ(0)
         ts(T.ff[:, :], B[2][:, 0:NP], 0.0, OP.is_equal, None, None, ["bk2"], ["ff"])
         ts(T.oh[:, :], B[2][:, 0:NP], 1.0, OP.max, T.cols[:, 2:3], OP.is_equal, ["bk2", "cols"], ["oh"])
         tt(T.fT[:, :], T.ff[:, :], T.Th[:, :], OP.mult, ["ff", "Th"], ["fT"])
+        sumx(1)
+        chunk(1)
+        summ(1)
+        if t > 0:
+            windows(t - 1, 6)
+            windows(t - 1, 7)
+            turned()
+        sumx(2)
         tt(T.ohc[:, :], T.oh[:, :], T.crep[:, :], OP.mult, ["oh", "crep"], ["ohc"])
-        ts(T.hoc[:, :], B[2][:, NP:2 * NP], T.SC[:, t:t + 1], OP.add, 16.0, OP.is_equal, ["bk2", "SC"], ["hoc"])
-        tt(T.x1[:, :], B[2][:, 384:396], T.bi[:, :], OP.add, ["bk2", "bi"], ["x1"])
-        tt(T.smi[:, 24:36], B[2][:, 396:408], T.x1[:, :], OP.add, ["bk2", "x1"], ["x2"])
-        ts(T.smi[:, 36:48], T.smi[:, 24:36], 4095, OP.bitwise_and, None, None, ["x2"], ["x3"])
-        cp(T.ql[:, :], T.smi[:, 36:48], ["x3"], ["ql"])
-        if not last:
-            ts(T.nd[:, :], B[2][:, 384:396], -1.0 / 256, OP.mult, 16.0, OP.add, ["bk2"], ["nd"])
-            empties()
-            tt(S(5), T.cf[:, :], S(1), OP.add, ["cf", "s1"], ["s5"])
-            ts(S(6), S(5), -8192.0, OP.add, None, None, ["s5"], ["s6"])
         pt = B[3][:, 0:NP]
         mm(pt, rot("Ih"), T.Th[:, :], True, False, ["Ih", "Th"], ["bk3"])
         mm(pt, rot("SI"), T.fT[:, :], False, False, ["SI", "fT"], ["bk3"])
         mm(pt, rot("E15"), T.ff[:, :], False, False, ["E15", "ff"], ["bk3"])
         mm(pt, rot("IN"), T.oh[:, :], False, False, ["IN", "oh"], ["bk3"])
         mm(pt, rot("Ih"), T.ohc[:, :], False, False, ["Ih", "ohc"], ["bk3"])
-        mm(B[6][:, 0:NP], T.B15[:, :], T.oneh[:, :], True, False, ["B15", "oneh"], ["bk6"])
-        mm(B[5][:, 0:12], T.Ih[:, 0:128], T.b16h[:, :], True, False, ["Ih", "b16h"], ["bk5"])
-        act(T.na[:, :], T.xc[:, :], AF.Copy, ["xc"], ["na"], scale=-1.0)
-        if t == 0:
-            act(T.lim[:, :], T.thr[:, :], AF.Copy, ["thr"], ["lim"])
-        else:
-            act(T.lim[:, :], T.thr[:, :], AF.Identity, ["thr", "a256"], ["lim"], bias=T.aa[:, 1:2])
-        chunk(2, True)
-        chunkp(2, True)
+        mm(B[2][:, 0:NP], MB(0), T.oneh[:, :], True, False, ["MB", "oneh"], ["bk2"])
+        pac = B[4][:, NP:2 * NP]
+        mm(pac, T.Ib[:, :], T.xc[:, :], True, False, ["Ib", "xc"], ["bk4"])
+        mm(pac, MB(7), T.oneh[:, :], False, False, ["MB", "oneh"], ["bk4"])
+        chunk(2)
+        summ(2)
+        if t > 0:
+            hand_end()
+        hand_begin(t)
 
         tt(T.ok[:, :], B[0][:, 0:NP], T.lim[:, :], OP.is_le, ["bk0", "lim"], ["ok"])
-        mm(B[4][:, 0:NP], T.TUi[:, :], T.ok[:, :], True, True, ["TUi", "ok"], ["bk4"])
-        mm(B[6][:, 0:NP], rot("TUr"), T.ok[:, :], False, True, ["TUr", "ok"], ["bk6"])
+        mm(B[1][:, 0:NP], T.TUi[:, :], T.ok[:, :], True, True, ["TUi", "ok"], ["bk1"])
+        mm(B[2][:, 0:NP], rot("TUr"), T.ok[:, :], False, True, ["TUr", "ok"], ["bk2"])
         mm(pt, rot("BH"), T.ok[:, :], False, True, ["BH", "ok"], ["bk3"])
-        mm(B[7][:, 0:NP], T.Ib[:, :], T.xc[:, :], True, False, ["Ib", "xc"], ["bk7"])
-        mm(B[7][:, 0:NP], T.Bac[:, :], T.oneh[:, :], False, False, ["Bac", "oneh"], ["bk7"])
-        ts(T.K1[:, :], B[4][:, 0:NP], 0.5, OP.is_ge, None, None, ["bk4"], ["K1"])
-        mm(B[7][:, 0:NP], T.B512[:, :], T.K1[:, :], False, True, ["B512", "K1"], ["bk7"])
-        diag(B[5][:, 0:12], "Wk", 0, "K1", 0, 1, ["K1"], "bk5", first=False)
-        mm(B[1][:, NP:2 * NP], T.B1[:, :], T.oneh[:, :], True, False, ["B1", "oneh"], ["bk1"])
-        mm(B[1][:, NP:2 * NP], T.Bh[:, :], T.K1[:, :], False, True, ["Bh", "K1"], ["bk1"])
-        if not last:
-            diag(B[0][:, 192:204], "Wr", 0, "K1", 0, 1, ["K1"], "bk0")
-        tt(T.fst[:, :], B[6][:, 0:NP], T.Trot[:, :], OP.max, ["bk6", "Trot"], ["fst"])
+        mm(B[0][:, 256:268], T.Ih[:, 0:128], T.b16h[:, :], True, False, ["Ih", "b16h"], ["bk0"])
+        ts(T.K1[:, :], B[1][:, 0:NP], 0.5, OP.is_ge, None, None, ["bk1"], ["K1"])
+        mm(pac, MB(2), T.K1[:, :], False, True, ["MB", "K1"], ["bk4"])
+        diag(B[0][:, 256:268], "Wk", "K1", 0, 1, ["K1"], "bk0", first=False)
+        tt(T.fst[:, :], B[2][:, 0:NP], T.Trot[:, :], OP.max, ["bk2", "Trot"], ["fst"])
         tt(T.Tc[:, :], B[3][:, 0:NP], T.fst[:, :], OP.min, ["bk3", "fst"], ["Tc"])
         if not last:
             to = T["TO%d" % t]
             nxt = T.cores[(rank + 1) % len(T.cores)]
             ts(to[:, :], T.Tc[:, :], 1536.0, OP.add, None, None, ["Tc"], ["TO%d" % t])
             rid, pid = topo.addr(nxt, core)
-            eng = topo.engines(core, nxt)[:8]
             mask = 0
-            for e in eng:
+            for e in send_engines(topo, core, nxt):
                 mask |= 1 << e
             op("G", lambda to=to, t=t, rid=rid, pid=pid, mask=mask: g.remote_dma(T["TT%d" % (t + 1)][:, :], to[:, :], T.sem["arr%d" % (t + 1)], T.sem.snd, pid, rid, mask),
                ["TO%d" % t], [], dma="snd")
-        tt(T.ac[:, :], B[7][:, 0:NP], T.na[:, :], OP.max, ["bk7", "na"], ["ac"])
-        cp(T.kl[:, :], B[5][:, 0:12], ["bk5"], ["kl"])
+        mm(B[1][:, NP:2 * NP], MB(4), T.oneh[:, :], True, False, ["MB", "oneh"], ["bk1"])
+        mm(B[1][:, NP:2 * NP], MB(3), T.K1[:, :], False, True, ["MB", "K1"], ["bk1"])
+        mm(B[3][:, 0:NP], MB(5), T.oneh[:, :], True, False, ["MB", "oneh"], ["bk3"])
+        mm(B[3][:, 0:NP], T.TU8[:, :], T.ok[:, :], False, False, ["TU8", "ok"], ["bk3"])
+        mm(B[3][:, 0:NP], MB(1), T.K1[:, :], False, True, ["MB", "K1"], ["bk3"])
+        mm(B[2][:, NP:2 * NP], T.BA[:, :], T.IH[:, NP:2 * NP], True, True, ["BA", "hinv"], ["bk2"])
+        tt(T.ac[:, :], B[4][:, NP:2 * NP], T.na[:, :], OP.max, ["bk4", "na"], ["ac"])
+        cp(T.kl[:, :], B[0][:, 256:268], ["bk0"], ["kl"])
         tt(T.vv[:, :], T.XT[:, :].indirect(T.kl[:, :]), T.ac[:, :], OP.add, ["XT0", "XT1", "XT2", "kl", "ac"], ["vv"])
         tt(T.uu[:, :], B[1][:, NP:2 * NP], T.vv[:, :], OP.mult, ["bk1", "vv"], ["uu"])
         act(T.au[:, :], T.uu[:, :], AF.Abs, ["uu"], ["au"])
+        tt(T.Tcap[:, :], B[3][:, 0:NP], T.Th[:, :], OP.max, ["bk3", "Th"], ["Tcap"])
+        diag(B[2][:, 384:408 if last else 420], "W256", "IH", 0, 2 if last else 3, ["inv", "hinv", "hfr"], "bk2")
         if not last:
-            tt(S(7), B[0][:, 192:204], T.nd[:, :], OP.mult, ["bk0", "nd"], ["s7"])
-            tt(S(8), S(7), B[5][:, 0:12], OP.subtract, ["s7", "bk5"], ["s8"])
+            diag(B[0][:, 192:204], "W0", "K1", 0, 1, ["K1"], "bk0")
         ts(T.y[:, :], T.au[:, :], RND, OP.add, -RND, OP.add, ["au"], ["y"])
-        diag(B[1][:, 0:12], "Ww", 0, "y", 0, 1, ["y"], "bk1")
+        diag(B[1][:, 0:12], "Ww", "y", 0, 1, ["y"], "bk1")
+        if t == 0:
+            matrices3()
+        tt(T.x1[:, :], B[2][:, 384:396], T.bi[:, :], OP.add, ["bk2", "bi"], ["x1"])
+        tt(T.smi[:, 24:36], B[2][:, 396:408], T.x1[:, :], OP.add, ["bk2", "x1"], ["x2"])
         if not last:
+            ts(T.nd[:, :], B[2][:, 384:396], -1.0 / 256, OP.mult, 16.0, OP.add, ["bk2"], ["nd"])
+            tt(S(7), B[0][:, 192:204], T.nd[:, :], OP.mult, ["bk0", "nd"], ["s7"])
+            tt(S(8), S(7), B[0][:, 256:268], OP.subtract, ["s7", "bk0"], ["s8"])
             op("V", lambda: g.vector.tensor_reduce(T.aa[:, 0:1], S(8), AxisListType.X, OP.add), ["s8"], ["ar"])
-            mm(B[0][:, 208:209], T.onesf[:, :], T.aa[:, 0:1], True, True, ["onesf", "ar"], ["bk0"])
+            empties(256.0)
+            mm(B[4][:, 0:1], T.onesf[:, :], T.aa[:, 0:1], True, True, ["onesf", "ar"], ["bk4"])
+            tt(S(5), T.cf[:, :], S(1), OP.add, ["cf", "s1"], ["s5"])
             ts(S(9), B[0][:, 192:204], -8192.0, OP.mult, None, None, ["bk0"], ["s9"])
-            tt(S(2), S(6), S(9), OP.subtract, ["s6", "s9"], ["s2"])
-            tt(S(3), S(0), S(2), OP.max, ["s0", "s2"], ["s3"])
-            tt(S(4), S(1), S(9), OP.add, ["s1", "s9"], ["s4"])
+            ts(S(6), S(5), -8192.0, OP.add, None, None, ["s5"], ["s6"])
         cp(T.zi[:, :], B[1][:, 0:12], ["bk1"], ["zi"])
         ts(T.zj[:, :], T.zi[:, :], 15, OP.bitwise_and, None, None, ["zi"], ["zj"])
         tt(T.zk[:, :], T.zj[:, :], T.b16i[:, :], OP.add, ["zj", "b16i"], ["zk"])
         cp(T.zl[:, :], T.zk[:, :], ["zk"], ["zl"])
         cp(T.X[:, :].indirect(T.zl[:, :]), T.y[:, :], ["y", "zl", "Xp"], ["X"])
         if not last:
-            ts(T.smi[:, 0:12], T.b37[:, 12 * t + 12:12 * t + 24], B[0][:, 208:209], OP.add, None, None, ["b37", "bk0"], ["fi"])
+            ts(T.smi[:, 0:12], T.b37[:, 12 * t + 12:12 * t + 24], B[4][:, 0:1], OP.add, None, None, ["b37", "bk4"], ["fi"])
+            tt(S(2), S(6), S(9), OP.subtract, ["s6", "s9"], ["s2"])
+            tt(S(4), S(1), S(9), OP.add, ["s1", "s9"], ["s4"])
             ts(T.smi[:, 12:24], T.smi[:, 0:12], 2047, OP.bitwise_and, None, None, ["fi"], ["fj"])
+            tt(S(3), S(0), S(2), OP.max, ["s0", "s2"], ["s3"])
             tt(S(5), S(4), T.smi[:, 12:24], OP.add, ["s4", "fj"], ["s5"])
             tt(T.cf[:, :], S(3), S(5), OP.max, ["s3", "s5"], ["cf"])
             cp(T.cl[:, :], T.cf[:, :], ["cf"], ["cl"])
-            ts(T.ai[:, 0:1], B[0][:, 208:209], float(CA), OP.add, None, None, ["bk0"], ["ai0"])
+            ts(T.ai[:, 0:1], B[4][:, 0:1], float(CA), OP.add, None, None, ["bk4"], ["ai0"])
             ts(T.ai[:, 1:2], T.ai[:, 0:1], 255, OP.bitwise_and, None, None, ["ai0"], ["ai1"])
             cp(T.aa[:, 1:2], T.ai[:, 1:2], ["ai1"], ["a256"])
-        if t == 0:
-            consts3()
-        mm(B[4][:, NP:2 * NP], T.B4k[:, :], T.oneh[:, :], True, False, ["B4k", "oneh"], ["bk4"])
-        mm(B[4][:, NP:2 * NP], T.TU8[:, :], T.ok[:, :], False, False, ["TU8", "ok"], ["bk4"])
-        mm(B[4][:, NP:2 * NP], T.B8n[:, :], T.K1[:, :], False, True, ["B8n", "K1"], ["bk4"])
-        mm(B[3][:, NP:2 * NP], T.B12k[:, :], T.oneh[:, :], True, False, ["B12k", "oneh"], ["bk3"])
-        mm(B[3][:, NP:2 * NP], T.I8n[:, :], T.hoc[:, :], False, False, ["I8n", "hoc"], ["bk3"])
-        mm(B[3][:, NP:2 * NP], T.B8n[:, :], T.K1[:, :], False, True, ["B8n", "K1"], ["bk3"])
-        tt(T.Tcap[:, :], B[4][:, NP:2 * NP], T.Th[:, :], OP.max, ["bk4", "Th"], ["Tcap"])
+        act(B[5][:, 0:NP], B[2][:, NP:2 * NP], AF.Identity, ["bk2", "WB"], ["bk5", "wall"], bias=T.WB[:, t:t + 1], scale=-4096.0)
+        ts(T.smi[:, 36:48], T.smi[:, 24:36], 4095, OP.bitwise_and, None, None, ["x2"], ["x3"])
+        ts(T.hoc[:, :], B[2][:, NP:2 * NP], T.SC[:, t:t + 1], OP.add, 16.0, OP.is_equal, ["bk2", "SC"], ["hoc"])
+        cp(T.ql[:, :], T.smi[:, 36:48], ["x3"], ["ql"])
+        mm(B[3][:, NP:2 * NP], MB(6), T.oneh[:, :], True, False, ["MB", "oneh"], ["bk3"])
+        mm(B[3][:, NP:2 * NP], MB(1), T.K1[:, :], False, False, ["MB", "K1"], ["bk3"])
+        for c in range(2):
+            windows(t, c)
+        mm(B[3][:, NP:2 * NP], T.I8n[:, :], T.hoc[:, :], False, True, ["I8n", "hoc"], ["bk3"])
+        for c in range(2, 8 if last else 6):
+            windows(t, c)
         tt(T.C1[:, :], B[3][:, NP:2 * NP], T.crep[:, :], OP.max, ["bk3", "crep"], ["C1"])
-        windows(t, 0, 8 if last else 4)
-        if last:
-            hand_end(t)
+        tt(B[5][:, NP:2 * NP], T.C1[:, :], T.Hp[:, :], OP.min, ["C1", "Hp"], ["bk5", "R3p"])
 
-    op("S", lambda: g.sync.dma_start(T.yx[:, :], T.X[:, 0:3072]), ["X"], [], dma="d_ox")
+    dma("S", "ox", T.yx[:, :], T.X[:, 0:3072], ["X"], [])
     ts(T.oya[:, :], T.Tc[:, :], 1536.0, OP.add, None, None, ["Tc"], ["oya"])
     ts(T.IH[:, 0:NP], T.Tc[:, :], EMPTY, OP.is_lt, None, None, ["Tc"], ["inv"])
     tt(T.oyt[:, :], T.oya[:, :], T.IH[:, 0:NP], OP.mult, ["oya", "inv"], ["oyt"])
-    store("S", "ot", T.yt[:, :], T.oyt[:, :], "oyt")
+    dma("S", "ot", T.yt[:, :], T.oyt[:, :], ["oyt"], [])
+    turned()
+    hand_end()
     ts(T.IH[:, NP:2 * NP], T.Hs[:, :], EMPTY, OP.is_lt, None, None, ["Hs"], ["hinv"])
-    mm(B[0][0:8, 0:2 * NP], T.M8[:, :], T.IH[:, :], True, True, ["M8", "inv", "hinv"], ["bk0"])
-    ts(T.SC[:, 0:1], T.SC[:, V - 1:V], 0.0, OP.add, None, None, ["SC"], ["SCx"])
-    ts(T.Bh[:, :], smb, T.SC[:, 0:1], OP.is_equal, None, None, ["smB", "SCx"], ["Bh"])
-    mm(B[1][:, 0:NP], T.Bh[:, :], T.Hs[:, :], True, True, ["Bh", "Hs"], ["bk1"])
+    mm(B[1][:, 0:NP], T.UR[:, :], T.Hs[:, :], True, True, ["UR", "Hs"], ["bk1"])
+    mm(B[0][0:8, 0:2 * NP], T.M8[:, :], T.IH[:, 0:2 * NP], True, True, ["M8", "inv", "hinv"], ["bk0"])
     ts(T.oyb[:, :], B[1][:, 0:NP], 1536.0, OP.add, None, None, ["bk1"], ["oyb"])
     ts(T.oya[:, :], B[1][:, 0:NP], EMPTY, OP.is_lt, None, None, ["bk1"], ["oya"])
     tt(T.oyh[:, :], T.oya[:, :], T.oyb[:, :], OP.mult, ["oya", "oyb"], ["oyh"])
+    dma("S", "oh", T.yh[:, :], T.oyh[:, :], ["oyh"], [])
     cp(T.omn[:, :], B[0][0:8, 0:2 * NP], ["bk0"], ["omn"])
-    store("S", "oh", T.yh[:, :], T.oyh[:, :], "oyh")
-    op("A", lambda: g.scalar.dma_start(T.yn[:, :], T.omn[:, 0:NP]), ["omn"], [], dma="d_on")
-    op("A", lambda: g.scalar.dma_start(T.ym[:, :], T.omn[:, NP:2 * NP]), ["omn"], [], dma="d_om")
+    dma("A", "on", T.yn[:, :], T.omn[:, 0:NP], ["omn"], [])
+    dma("A", "om", T.ym[:, :], T.omn[:, NP:2 * NP], ["omn"], [])
 
     emit(g, core, T, topo, ops, rank)
 
@@ -450,17 +463,12 @@ def rank_program(g, core, T, topo):
 def emit(g, core, T, topo, ops, rank):
     Q = {"V": g.vector, "A": g.scalar, "P": g.tensor, "G": g, "S": g.sync}
     sems = {"V": "qV", "A": "qA", "P": "qP", "G": "qG"}
-    seq = {}
+    seq, pos = {}, {}
     for k, o in enumerate(ops):
-        seq.setdefault(o["q"], []).append(k)
-    pos = {}
-    for q in seq:
-        for i, k in enumerate(seq[q]):
-            pos[k] = i
+        pos[k] = len(seq.setdefault(o["q"], []))
+        seq[o["q"]].append(k)
     know = {q: ({}, set()) for q in "VAPGS"}
-    after = {}
-    needed = set()
-    waits = {}
+    after, needed, waits = {}, set(), {}
     for k, o in enumerate(ops):
         q = o["q"]
         if q == "R":
@@ -468,49 +476,43 @@ def emit(g, core, T, topo, ops, rank):
             continue
         kn, kd = know[q]
         wl = []
-        need = {}
-        for d in sorted(o["deps"], reverse=True):
-            od = ops[d]
-            if od["dma"]:
-                if d not in kd:
-                    wl.append(d)
-                    kd.add(d)
-                    kn2, kd2 = after[d]
-                    for a in kn2:
-                        kn[a] = max(kn.get(a, -1), kn2[a])
-                    kd |= kd2
-            else:
-                if kn.get(od["q"], -1) < pos[d]:
-                    need[od["q"]] = max(need.get(od["q"], -1), pos[d])
-        for q2 in sorted(need, key=lambda a: -seq[a][need[a]]):
-            p = need[q2]
-            if kn.get(q2, -1) >= p:
-                continue
-            d = seq[q2][p]
+
+        def learn(d):
             wl.append(d)
-            needed.add(d)
-            kn[q2] = p
             kn2, kd2 = after[d]
             for a in kn2:
                 kn[a] = max(kn.get(a, -1), kn2[a])
-            kd |= kd2
+            kd.update(kd2)
+
+        need = {}
+        for d in sorted(o["deps"], reverse=True):
+            od = ops[d]
+            if not od["dma"]:
+                need[od["q"]] = max(need.get(od["q"], -1), pos[d])
+            elif d not in kd:
+                kd.add(d)
+                learn(d)
+        for q2 in sorted(need, key=lambda a: -seq[a][need[a]]):
+            p = need[q2]
+            if kn.get(q2, -1) < p:
+                kn[q2] = p
+                needed.add(seq[q2][p])
+                learn(seq[q2][p])
         waits[k] = wl
         after[k] = (dict(kn), set(kd))
     for q in "VAPG":
-        if q in seq:
-            comp = [k for k in seq[q] if not ops[k]["dma"]]
-            if comp:
-                needed.add(comp[-1])
+        comp = [k for k in seq.get(q, []) if not ops[k]["dma"]]
+        if comp:
+            needed.add(comp[-1])
     count = {}
     cnt = {q: 0 for q in "VAPG"}
     for k, o in enumerate(ops):
         if k in needed:
             cnt[o["q"]] += 1
             count[k] = cnt[o["q"]]
-    prev = T.cores[(rank - 1) % len(T.cores)]
-    ein = len(topo.engines(prev, core)[:8])
-    nxt = T.cores[(rank + 1) % len(T.cores)]
-    eout = len(topo.engines(core, nxt)[:8])
+    n = len(T.cores)
+    ein = len(send_engines(topo, T.cores[(rank - 1) % n], core))
+    eout = len(send_engines(topo, core, T.cores[(rank + 1) % n]))
     nsend = 0
     for k, o in enumerate(ops):
         q = o["q"]

@@ -6,7 +6,7 @@ V = 6
 NP = 192
 CW = 3088
 EMPTY = 1536.0
-PARTS = ("MX", "cols", "Wr", "b", "RW", "WIN", "MB")
+PARTS = ("MX", "cols", "b", "RW", "RA", "WIN", "WINA", "MB")
 CA = 8 * 16 * (191 * 192 // 2)
 RND = 8388608.0
 
@@ -16,7 +16,9 @@ SCRATCH = {
     "MX": ("sbuf", [128, 3072], "bfloat16"),
     "IOT": ("sbuf", [128, 3072], "float32"),
     "WIN": ("sbuf", [128, 4096], "float32"),
-    "RW": ("sbuf", [128, 16 * 128], "float16"),
+    "WINA": ("sbuf", [128, 1024], "float32"),
+    "RW": ("sbuf", [128, 16 * 128], "float16"), "RA": ("sbuf", [128, 4 * 128], "float16"), "Tg": ("sbuf", [128, NP], "float16"),
+    "qm": ("sbuf", [128, 12], "uint16"),
     "nmi": ("sbuf", [8, 576], "int32"), "nmf": ("sbuf", [8, 576], "float32"), "R8": ("sbuf", [8, 128], "float32"),
     "tri": ("sbuf", [128, NP], "int32"), "hai": ("sbuf", [128, NP], "int32"), "wti": ("sbuf", [128, 1], "int32"),
     "smB": ("sbuf", [128, 272], "bfloat16"), "smC": ("sbuf", [128, 256], "bfloat16"), "smA": ("sbuf", [128, 256], "bfloat16"),
@@ -37,18 +39,19 @@ SCRATCH = {
     "thr": ("sbuf", [128, NP], "float32"), "lim": ("sbuf", [128, NP], "float32"),
     "Th": ("sbuf", [128, NP], "float16"), "IH": ("sbuf", [128, 3 * NP], "float16"), "Hs": ("sbuf", [128, NP], "float16"),
     "Hp": ("sbuf", [128, NP], "float16"), "ff": ("sbuf", [128, NP], "float16"), "oh": ("sbuf", [128, NP], "float16"),
-    "fT": ("sbuf", [128, NP], "float16"), "ohc": ("sbuf", [128, NP], "float16"), "crep": ("sbuf", [128, NP], "float32"),
-    "Trot": ("sbuf", [128, NP], "float32"), "xc": ("sbuf", [128, NP], "bfloat16"), "na": ("sbuf", [128, NP], "float32"),
+    "fT": ("sbuf", [128, NP], "float16"), "ohc": ("sbuf", [128, NP], "float16"), "crep0": ("sbuf", [128, NP], "float32"),
+    "crep1": ("sbuf", [128, NP], "float32"),
+    "Trot": ("sbuf", [128, NP], "float32"), "xc": ("sbuf", [128, NP], "bfloat16"), "na": ("sbuf", [128, NP], "bfloat16"),
     "ok": ("sbuf", [128, NP], "float16"), "K1": ("sbuf", [128, NP], "float16"), "fst": ("sbuf", [128, NP], "float16"),
     "Tc": ("sbuf", [128, NP], "float16"), "ac": ("sbuf", [128, NP], "float32"), "vv": ("sbuf", [128, NP], "float32"),
     "uu": ("sbuf", [128, NP], "float32"), "au": ("sbuf", [128, NP], "float32"), "y": ("sbuf", [128, NP], "bfloat16"),
     "Tcap": ("sbuf", [128, NP], "float16"), "hoc": ("sbuf", [128, NP], "float16"),
-    "C1": ("sbuf", [128, NP], "float32"), "Rv": ("sbuf", [128, NP], "float32"), "R2": ("sbuf", [128, NP], "float32"),
+    "Rv": ("sbuf", [128, NP], "float32"), "R2": ("sbuf", [128, NP], "float32"),
     "cf": ("sbuf", [128, 12], "float32"), "cl": ("sbuf", [128, 12], "uint16"), "kl": ("sbuf", [128, 12], "uint16"),
     "zl": ("sbuf", [128, 12], "uint16"), "ql": ("sbuf", [128, 12], "uint16"),
     "zi": ("sbuf", [128, 12], "int32"), "zj": ("sbuf", [128, 12], "int32"), "zk": ("sbuf", [128, 12], "int32"),
     "x1": ("sbuf", [128, 12], "float32"), "nd": ("sbuf", [128, 12], "float32"),
-    "sm": ("sbuf", [128, 12 * 10], "float32"), "smi": ("sbuf", [128, 12 * 4], "int32"),
+    "sm": ("sbuf", [128, 12 * 10], "float32"), "smi": ("sbuf", [128, 12 * 5], "int32"),
     "aa": ("sbuf", [128, 4], "float32"), "ai": ("sbuf", [128, 2], "int32"),
     "oyh": ("sbuf", [128, NP], "float32"), "oyt": ("sbuf", [128, NP], "float32"), "oya": ("sbuf", [128, NP], "float32"),
     "oyb": ("sbuf", [128, NP], "float32"), "omn": ("sbuf", [8, 2 * NP], "float32"),
@@ -190,14 +193,21 @@ def rank_program(g, core, T, topo):
     ts(T.WB[:, :], T.SC[:, :], -4096.0, OP.mult, 4096.0 * 16.5, OP.add, ["SC"], ["WB"])
     ts(T.W0[:, :], smp, 0.0, OP.is_equal, T.E0[:, 0:1], OP.mult, ["smB", "smBp", "E0"], ["W0"])
 
+    ts(T.Ib[:, :], smb, SP, OP.is_equal, None, None, ["smB", "SC"], ["Ib"])
+    ts(T.NB[:, :], smb, 0.0, OP.is_ge, -1.0, OP.mult, ["smB"], ["NB"])
+    ts(T.W2[:, :], smp, 0.0, OP.is_equal, 2.0, OP.mult, ["smB", "smBp"], ["W2"])
+    ts(T.WN[:, :], smp, 0.0, OP.is_equal, -1.0, OP.mult, ["smB", "smBp"], ["WN"])
+    ts(T.BA[:, :], smb, 0.0, OP.is_ge, None, None, ["smB"], ["BA"])
+    ts(T.I8[:, :], smb, SP, OP.is_equal, 8192.0, OP.mult, ["smB", "SC"], ["I8"])
+    ts(T.Ih[:, :], smb2, SP, OP.is_equal, None, None, ["smB", "SC"], ["Ih"])
+
     def spread(j, nm, b):
         cp(T.nmf[:, NP * j:NP * j + NP], T.nmi[:, NP * j:NP * j + NP], [nm], [nm + "f"])
         mm(B[b][:, 0:NP], T.R8[:, :], T.nmf[:, NP * j:NP * j + NP], True, True, ["R8", nm + "f"], ["bk%d" % b])
 
     spread(1, "nmi_m", 4)
     ts(T.bi[:, :], T.iq[:, :], SP, OP.add, None, None, ["iq", "SC"], ["bi"])
-    for t in range(V):
-        ts(T.b37[:, 12 * t:12 * t + 12], T.bi[:, :], 37.0, OP.mult, float(613 * t + (CA if t else 0)), OP.add, ["bi"], ["b37"])
+    ts(T.b37[:, 0:12], T.bi[:, :], 37.0, OP.mult, None, None, ["bi"], ["b37"])
     ts(T.oyt[:, :], B[4][:, 0:NP], SP, OP.is_le, 3072.0, OP.mult, ["bk4", "SC"], ["tb"])
     tt(T.oyb[:, :], T.oyt[:, :], T.hai[:, :], OP.max, ["tb", "hai"], ["h0f"])
     ts(T.Hs[:, :], T.oyb[:, :], -1536.0, OP.add, None, None, ["h0f"], ["Hs"])
@@ -209,26 +219,17 @@ def rank_program(g, core, T, topo):
 
     def empties(scale):
         pd = B[2][:, 408:420]
-        ts(S(2), pd, EMPTY * scale, OP.is_ge, -8192.0, OP.mult, ["bk2"], ["s2"])
-        ts(S(3), pd, 1.0 / scale, OP.mult, 1536.0, OP.add, ["bk2"], ["s3"])
-        ts(S(1), S(2), -1.0, OP.mult, -8192.0, OP.add, ["s2"], ["s1"])
-        tt(S(0), S(3), S(2), OP.add, ["s2", "s3"], ["s0"])
+        ts(S(1), pd, EMPTY * scale, OP.is_lt, 4096.0, OP.mult, ["bk2"], ["s1"])
+        ts(S(0), pd, 1.0 / scale, OP.mult, 1536.0, OP.add, ["bk2"], ["s0"])
 
     empties(1.0)
     cp(T.smi[:, 0:12], T.b37[:, 0:12], ["b37"], ["fi"])
     ts(T.smi[:, 12:24], T.smi[:, 0:12], 2047, OP.bitwise_and, None, None, ["fi"], ["fj"])
-    tt(S(4), S(1), T.smi[:, 12:24], OP.add, ["fj", "s1"], ["s4"])
-    tt(T.cf[:, :], S(0), S(4), OP.max, ["s0", "s4"], ["cf"])
+    tt(S(4), S(1), T.smi[:, 12:24], OP.max, ["fj", "s1"], ["s4"])
+    tt(T.cf[:, :], S(0), S(4), OP.min, ["s0", "s4"], ["cf"])
     cp(T.cl[:, :], T.cf[:, :], ["cf"], ["cl"])
 
     def matrices():
-        ts(T.Ib[:, :], smb, SP, OP.is_equal, None, None, ["smB", "SC"], ["Ib"])
-        ts(T.NB[:, :], smb, 0.0, OP.is_ge, -1.0, OP.mult, ["smB"], ["NB"])
-        ts(T.W2[:, :], smp, 0.0, OP.is_equal, 2.0, OP.mult, ["smB", "smBp"], ["W2"])
-        ts(T.WN[:, :], smp, 0.0, OP.is_equal, -1.0, OP.mult, ["smB", "smBp"], ["WN"])
-        ts(T.BA[:, :], smb, 0.0, OP.is_ge, None, None, ["smB"], ["BA"])
-        ts(T.I8[:, :], smb, SP, OP.is_equal, 8192.0, OP.mult, ["smB", "SC"], ["I8"])
-        ts(T.Ih[:, :], smb2, SP, OP.is_equal, None, None, ["smB", "SC"], ["Ih"])
         ts(T.SI[:, :], smb2, T.cols[:, 1:2], OP.is_equal, None, None, ["smB", "cols"], ["SI"])
         ts(T.E15[:, :], smb2, 15.0, OP.is_equal, T.cols[:, 3:4], OP.mult, ["smB", "cols"], ["E15"])
         tt(T.SI[:, :], T.SI[:, :], T.Ih[:, :], OP.subtract, ["SI", "Ih"], ["SI"])
@@ -239,6 +240,8 @@ def rank_program(g, core, T, topo):
         ts(T.BH[:, :], smb2, 0.0, OP.is_ge, 8192.0, OP.mult, ["smB"], ["BH"])
         for j in range(len(row0)):
             ts(MB(j), smb, 0.0, OP.is_ge, T.cols[:, 3 + j:4 + j], OP.mult, ["smB", "cols"], ["MB"])
+        for t in range(1, V):
+            ts(T.b37[:, 12 * t:12 * t + 12], T.bi[:, :], 37.0, OP.mult, float(613 * t + CA), OP.add, ["bi"], ["b37"])
         ts(T.b16h[:, :], T.bi[:, :], 16.0, OP.mult, None, None, ["bi"], ["b16h"])
         ts(T.Wk[:, :], smp, 0.0, OP.is_equal, T.cols[:, 0:1], OP.mult, ["smB", "smBp", "cols"], ["Wk"])
         ts(T.W256[:, :], smp, 0.0, OP.is_equal, 256.0, OP.mult, ["smB", "smBp"], ["W256"])
@@ -250,27 +253,51 @@ def rank_program(g, core, T, topo):
         ts(T.I8n[:, :], smb, SP, OP.is_equal, -4096.0, OP.mult, ["smB", "SC"], ["I8n"])
         ts(T.Ww[:, :], smp, 0.0, OP.is_equal, T.cols[:, 12:13], OP.mult, ["smB", "smBp", "wtf"], ["Ww"])
 
+        for w in range(4):
+            ts(T.RA[:, 128 * w:128 * w + 128], smb, T.SC[:, 15 - w:16 - w], OP.is_equal, None, None, ["smB", "SC"], ["RA"])
+
     def matrices3():
         for w in range(16):
             ts(T.RW[:, 128 * w:128 * w + 128], smb, T.cw[:, w:w + 1], OP.is_equal, None, None, ["smB", "cw"], ["RW"])
         ts(T.M8[:, :], T.smB[:, 16:144:16], 0.0, OP.is_ge, None, None, ["smB"], ["M8"])
         ts(T.UR[:, :], smb, T.SC[:, V - 1:V], OP.is_equal, None, None, ["smB", "SC"], ["UR"])
 
-    matrices()
-    spread(2, "nmi_t", 6)
-    act(T.thr[:, :], B[6][:, 0:NP], AF.Copy, ["bk6"], ["thr"])
-    matrices2()
 
-    def windows(t, c):
-        b = 6 + c % 2
-        for h in range(2):
-            o = 2 * c + h
-            w = (t + 1 - o) % 16
-            mm(B[b][:, 256 * h:256 * h + NP], T.RW[:, 128 * w:128 * w + 128], T.Tcap[:, :], True, True, ["RW", "Tcap"], ["bk%d" % b])
-        act(T.WIN[:, 512 * c:512 * c + 448], B[b][:, 0:448], AF.Copy, ["bk%d" % b], ["WIN"])
+    def turn1():
+        for c in range(2):
+            for h in range(2):
+                w = 2 * c + h
+                mm(B[6 + c][:, 256 * h:256 * h + NP], T.RA[:, 128 * w:128 * w + 128], T.Tcap[:, :], True, True, ["RA", "Tcap"], ["bk%d" % (6 + c)])
+            act(T.WINA[:, 512 * c:512 * c + 448], B[6 + c][:, 0:448], AF.Copy, ["bk%d" % (6 + c)], ["WINA"])
+
+    def turn2(t):
+        cp(T.Tg[:, :], T.WINA[:, :].indirect(T.ql[:, :]), ["WINA", "ql"], ["Tg"])
+        for c in range(2):
+            for h in range(2):
+                w = (t + 1 - 4 * (2 * c + h)) % 16
+                mm(B[6 + c][:, 256 * h:256 * h + NP], T.RW[:, 128 * w:128 * w + 128], T.Tg[:, :], True, True, ["RW", "Tg"], ["bk%d" % (6 + c)])
 
     def turned():
-        act(T.Rv[:, :], T.WIN[:, :].indirect(T.ql[:, :]), AF.Copy, ["WIN", "ql"], ["Rv"])
+        for c in range(2):
+            for h in range(2):
+                o = 1024 * (2 * c + h)
+                act(T.WIN[:, o:o + NP], B[6 + c][:, 256 * h:256 * h + NP], AF.Copy, ["bk%d" % (6 + c)], ["WIN"])
+        act(T.Rv[:, :], T.WIN[:, :].indirect(T.qm[:, :]), AF.Copy, ["WIN", "qm"], ["Rv"])
+
+    def lists():
+        tt(T.x1[:, :], B[2][:, 384:396], T.bi[:, :], OP.add, ["bk2", "bi"], ["x1"])
+        tt(T.smi[:, 24:36], B[2][:, 396:408], T.x1[:, :], OP.add, ["bk2", "x1"], ["x2"])
+        ts(T.smi[:, 36:48], T.smi[:, 24:36], 1023, OP.bitwise_and, None, None, ["x2"], ["x3"])
+        ts(T.smi[:, 48:60], T.smi[:, 24:36], 3072 + 255, OP.bitwise_and, None, None, ["x2"], ["x4"])
+        cp(T.ql[:, :], T.smi[:, 36:48], ["x3"], ["ql"])
+        cp(T.qm[:, :], T.smi[:, 48:60], ["x4"], ["qm"])
+
+    def card_c(t):
+        ts(T.hoc[:, :], B[2][:, NP:2 * NP], T.SC[:, t:t + 1], OP.add, 16.0, OP.is_equal, ["bk2", "SC"], ["hoc"])
+        mm(B[3][:, NP:2 * NP], T.I8n[:, :], T.hoc[:, :], False, True, ["I8n", "hoc"], ["bk3"])
+
+    def card_c2(t):
+        tt(B[5][:, NP:2 * NP], B[3][:, NP:2 * NP], T["crep%d" % (t % 2)][:, :], OP.max, ["bk3", "crep%d" % (t % 2)], ["bk5", "C1"])
 
     def hand_end():
         tt(T.R2[:, :], B[5][:, 0:NP], T.Rv[:, :], OP.max, ["Rv", "bk5", "wall"], ["R2"])
@@ -282,6 +309,7 @@ def rank_program(g, core, T, topo):
         if t < V - 1:
             ts(T.IH[:, 2 * NP:3 * NP], T.Hp[:, :], T.E0[:, t + 1:t + 2], OP.mult, None, None, ["Hp", "E0"], ["hfr"])
 
+    cp(T.xc[:, :], T.X[:, :].indirect(T.cl[:, :]), ["X", "Xp", "cl"], ["xc"])
     for t in range(V):
         last = t == V - 1
         tn = "TT%d" % t
@@ -293,69 +321,92 @@ def rank_program(g, core, T, topo):
             return T[nm][:, ro:ro + 128] if jj else T[nm][:, 0:128]
 
         def chunk(c):
-            for s in range(16):
-                tt(T.MX[:, 1024 * c + s:1024 * c + 1024:16], B[1][:, 64 * c:64 * c + 64], T.XT[:, 1024 * c + s:1024 * c + 1024:16], OP.max,
-                   ["bk1", "XT%d" % c], ["MX%d_%d" % (c, s // 4)])
+            for s in range(4):
+                o = 256 * (c % 2)
+                tt(T.MX[:, 1024 * c + s:1024 * c + 1024:4], B[1][:, o:o + 256], T.XT[:, 1024 * c + s:1024 * c + 1024:4], OP.max,
+                   ["bk1", "XT%d" % c], ["MX%d_%d" % (c, s)])
+
+        def fours(c, n):
+            for s in range(4):
+                mm(B[1][:, s:256 * n:4], T.Ib[:, :], T.xc[:, 64 * c:64 * c + 64 * n], True, True, ["Ib", "xc"], ["bk1"])
 
         def sumx(c):
             for s in range(16):
                 mm(B[0][:, 64 * c:64 * c + 64], T.WN[:, 16 - s:144 - s], T.XT[:, 1024 * c + s:1024 * c + 1024:16], False, False, ["WN", "XT%d" % c], ["bk0"])
 
         def summ(c):
-            for s in range(16):
-                mm(B[0][:, 64 * c:64 * c + 64], T.W2[:, 16 - s:144 - s], T.MX[:, 1024 * c + s:1024 * c + 1024:16], False, c == 2 and s == 15,
-                   ["W2", "MX%d_%d" % (c, s // 4)], ["bk0"])
+            for k in range(16):
+                s = k // 4 + 4 * (k % 4)
+                mm(B[0][:, 64 * c:64 * c + 64], T.W2[:, 16 - s:144 - s], T.MX[:, 1024 * c + s:1024 * c + 1024:16], False, c == 2 and k == 15,
+                   ["W2", "MX%d_%d" % (c, s % 4)], ["bk0"])
 
         if t > 0:
             op("R", None, [], [tn], dma="arr%d" % t)
-        cp(T.XT[:, 0:1024], T.X[:, :].indirect(tab[:, 0:64]), ["X", "Xp", tn], ["XT0"])
-        act(T.xc[:, :], T.X[:, :].indirect(T.cl[:, :]), AF.Copy, ["X", "Xp", "cl"], ["xc"])
-        for c in (1, 2):
+        cp(T.xc[:, :], T.X[:, :].indirect(T.cl[:, :]), ["X", "Xp", "cl"], ["xc"])
+        def gather(c):
             act(T.XT[:, 1024 * c:1024 * c + 1024], T.X[:, :].indirect(tab[:, 64 * c:64 * c + 64]), AF.Copy, ["X", "Xp", tn], ["XT%d" % c])
-        act(T.crep[:, :], T.IOT[:, :].indirect(T.cl[:, :]), AF.Copy, ["IOT", "cl"], ["crep"])
+
+        crn = "crep%d" % (t % 2)
+        fours(0, 2)
+        mm(B[0][:, 0:NP], T.NB[:, :], T.xc[:, :], True, False, ["NB", "xc"], ["bk0"])
+        if t > 0:
+            lists()
+            ts(T.ai[:, 0:1], B[4][:, 0:1], float(CA), OP.add, None, None, ["bk4"], ["ai0"])
+            ts(T.ai[:, 1:2], T.ai[:, 0:1], 255, OP.bitwise_and, None, None, ["ai0"], ["ai1"])
+            cp(T.aa[:, 1:2], T.ai[:, 1:2], ["ai1"], ["a256"])
+            card_c(t - 1)
         ts(T.Th[:, :], tab[:, :], -1536.0, OP.add, None, None, [tn], ["Th"])
         ts(T.IH[:, 0:NP], tab[:, :], 3072.0, OP.is_ge, None, None, [tn], ["inv"])
-        mm(B[1][:, 0:NP], T.Ib[:, :], T.xc[:, :], True, True, ["Ib", "xc"], ["bk1"])
-        mm(B[0][:, 0:NP], T.NB[:, :], T.xc[:, :], True, False, ["NB", "xc"], ["bk0"])
-        mm(B[0][:, 0:NP], T.I8[:, :], T.IH[:, 0:NP], False, False, ["I8", "inv"], ["bk0"])
+        ts(T.na[:, :], T.xc[:, :], -1.0, OP.mult, None, None, ["xc"], ["na"])
+        gather(0)
         mm(B[2][:, 0:NP], T.BA[:, :], T.IH[:, 0:NP], True, True, ["BA", "inv"], ["bk2"])
+        mm(B[4][:, 0:NP], rot("Ih"), T.Th[:, :], True, True, ["Ih", "Th"], ["bk4"])
+        mm(B[0][:, 0:NP], T.I8[:, :], T.IH[:, 0:NP], False, False, ["I8", "inv"], ["bk0"])
         sumx(0)
-        mm(B[3][:, NP:2 * NP], rot("Ih"), T.Th[:, :], True, True, ["Ih", "Th"], ["bk3"])
-        act(T.Trot[:, :], B[3][:, NP:2 * NP], AF.Copy, ["bk3"], ["Trot"])
-        act(T.na[:, :], T.xc[:, :], AF.Copy, ["xc"], ["na"], scale=-1.0)
+        chunk(0)
+        summ(0)
         if t == 0:
+            spread(2, "nmi_t", 6)
+            matrices()
+            matrices2()
+        gather(1)
+        act(T.Trot[:, :], B[4][:, 0:NP], AF.Copy, ["bk4"], ["Trot"])
+        act(T[crn][:, :], T.IOT[:, :].indirect(T.cl[:, :]), AF.Copy, ["IOT", "cl"], [crn])
+        gather(2)
+        if t == 0:
+            act(T.thr[:, :], B[6][:, 0:NP], AF.Copy, ["bk6"], ["thr"])
             act(T.lim[:, :], T.thr[:, :], AF.Copy, ["thr"], ["lim"])
         else:
             act(T.lim[:, :], T.thr[:, :], AF.Identity, ["thr", "a256"], ["lim"], bias=T.aa[:, 1:2])
-        chunk(0)
-        summ(0)
+        if t > 0:
+            card_c2(t - 1)
+            tt(B[5][:, NP:2 * NP], B[5][:, NP:2 * NP], T.Hp[:, :], OP.min, ["C1", "bk5", "Hp"], ["bk5", "R3p"])
+        mm(B[7][:, 0:NP], T.Ih[:, 0:128], T.Th[:, :], True, True, ["Ih", "Th"], ["bk7"])
+        sumx(1)
         ts(T.ff[:, :], B[2][:, 0:NP], 0.0, OP.is_equal, None, None, ["bk2"], ["ff"])
         ts(T.oh[:, :], B[2][:, 0:NP], 1.0, OP.max, T.cols[:, 2:3], OP.is_equal, ["bk2", "cols"], ["oh"])
-        tt(T.fT[:, :], T.ff[:, :], T.Th[:, :], OP.mult, ["ff", "Th"], ["fT"])
-        sumx(1)
-        chunk(1)
-        summ(1)
-        if t > 0:
-            windows(t - 1, 6)
-            windows(t - 1, 7)
-            turned()
-        sumx(2)
-        tt(T.ohc[:, :], T.oh[:, :], T.crep[:, :], OP.mult, ["oh", "crep"], ["ohc"])
+        tt(T.fT[:, :], B[7][:, 0:NP], T.ff[:, :], OP.mult, ["ff", "bk7"], ["fT"])
         pt = B[3][:, 0:NP]
         mm(pt, rot("Ih"), T.Th[:, :], True, False, ["Ih", "Th"], ["bk3"])
-        mm(pt, rot("SI"), T.fT[:, :], False, False, ["SI", "fT"], ["bk3"])
         mm(pt, rot("E15"), T.ff[:, :], False, False, ["E15", "ff"], ["bk3"])
         mm(pt, rot("IN"), T.oh[:, :], False, False, ["IN", "oh"], ["bk3"])
-        mm(pt, rot("Ih"), T.ohc[:, :], False, False, ["Ih", "ohc"], ["bk3"])
+        mm(pt, rot("SI"), T.fT[:, :], False, False, ["SI", "fT"], ["bk3"])
         mm(B[2][:, 0:NP], MB(0), T.oneh[:, :], True, False, ["MB", "oneh"], ["bk2"])
         pac = B[4][:, NP:2 * NP]
         mm(pac, T.Ib[:, :], T.xc[:, :], True, False, ["Ib", "xc"], ["bk4"])
         mm(pac, MB(7), T.oneh[:, :], False, False, ["MB", "oneh"], ["bk4"])
+        if t > 0:
+            turn2(t - 1)
+        chunk(1)
+        summ(1)
+        fours(2, 1)
+        if t > 0:
+            turned()
+        tt(T.ohc[:, :], T.oh[:, :], T[crn][:, :], OP.mult, ["oh", crn], ["ohc"])
+        sumx(2)
+        mm(pt, rot("Ih"), T.ohc[:, :], False, False, ["Ih", "ohc"], ["bk3"])
         chunk(2)
         summ(2)
-        if t > 0:
-            hand_end()
-        hand_begin(t)
 
         tt(T.ok[:, :], B[0][:, 0:NP], T.lim[:, :], OP.is_le, ["bk0", "lim"], ["ok"])
         mm(B[1][:, 0:NP], T.TUi[:, :], T.ok[:, :], True, True, ["TUi", "ok"], ["bk1"])
@@ -382,69 +433,62 @@ def rank_program(g, core, T, topo):
         mm(B[3][:, 0:NP], MB(5), T.oneh[:, :], True, False, ["MB", "oneh"], ["bk3"])
         mm(B[3][:, 0:NP], T.TU8[:, :], T.ok[:, :], False, False, ["TU8", "ok"], ["bk3"])
         mm(B[3][:, 0:NP], MB(1), T.K1[:, :], False, True, ["MB", "K1"], ["bk3"])
-        mm(B[2][:, NP:2 * NP], T.BA[:, :], T.IH[:, NP:2 * NP], True, True, ["BA", "hinv"], ["bk2"])
         tt(T.ac[:, :], B[4][:, NP:2 * NP], T.na[:, :], OP.max, ["bk4", "na"], ["ac"])
+        if t > 0:
+            hand_end()
         cp(T.kl[:, :], B[0][:, 256:268], ["bk0"], ["kl"])
         tt(T.vv[:, :], T.XT[:, :].indirect(T.kl[:, :]), T.ac[:, :], OP.add, ["XT0", "XT1", "XT2", "kl", "ac"], ["vv"])
         tt(T.uu[:, :], B[1][:, NP:2 * NP], T.vv[:, :], OP.mult, ["bk1", "vv"], ["uu"])
         act(T.au[:, :], T.uu[:, :], AF.Abs, ["uu"], ["au"])
         tt(T.Tcap[:, :], B[3][:, 0:NP], T.Th[:, :], OP.max, ["bk3", "Th"], ["Tcap"])
-        diag(B[2][:, 384:408 if last else 420], "W256", "IH", 0, 2 if last else 3, ["inv", "hinv", "hfr"], "bk2")
         if not last:
             diag(B[0][:, 192:204], "W0", "K1", 0, 1, ["K1"], "bk0")
+        turn1()
         ts(T.y[:, :], T.au[:, :], RND, OP.add, -RND, OP.add, ["au"], ["y"])
         diag(B[1][:, 0:12], "Ww", "y", 0, 1, ["y"], "bk1")
-        if t == 0:
-            matrices3()
-        tt(T.x1[:, :], B[2][:, 384:396], T.bi[:, :], OP.add, ["bk2", "bi"], ["x1"])
-        tt(T.smi[:, 24:36], B[2][:, 396:408], T.x1[:, :], OP.add, ["bk2", "x1"], ["x2"])
+        hand_begin(t)
+        mm(B[2][:, NP:2 * NP], T.BA[:, :], T.IH[:, NP:2 * NP], True, True, ["BA", "hinv"], ["bk2"])
+        diag(B[2][:, 384:408 if last else 420], "W256", "IH", 0, 2 if last else 3, ["inv", "hinv", "hfr"], "bk2")
         if not last:
-            ts(T.nd[:, :], B[2][:, 384:396], -1.0 / 256, OP.mult, 16.0, OP.add, ["bk2"], ["nd"])
-            tt(S(7), B[0][:, 192:204], T.nd[:, :], OP.mult, ["bk0", "nd"], ["s7"])
-            tt(S(8), S(7), B[0][:, 256:268], OP.subtract, ["s7", "bk0"], ["s8"])
-            op("V", lambda: g.vector.tensor_reduce(T.aa[:, 0:1], S(8), AxisListType.X, OP.add), ["s8"], ["ar"])
-            empties(256.0)
-            mm(B[4][:, 0:1], T.onesf[:, :], T.aa[:, 0:1], True, True, ["onesf", "ar"], ["bk4"])
-            tt(S(5), T.cf[:, :], S(1), OP.add, ["cf", "s1"], ["s5"])
-            ts(S(9), B[0][:, 192:204], -8192.0, OP.mult, None, None, ["bk0"], ["s9"])
-            ts(S(6), S(5), -8192.0, OP.add, None, None, ["s5"], ["s6"])
+            tt(S(5), B[0][:, 192:204], T.cf[:, :], OP.mult, ["bk0", "cf"], ["s5"])
+            ts(S(9), B[0][:, 192:204], -4096.0, OP.mult, 4096.0, OP.add, ["bk0"], ["s9"])
         cp(T.zi[:, :], B[1][:, 0:12], ["bk1"], ["zi"])
         ts(T.zj[:, :], T.zi[:, :], 15, OP.bitwise_and, None, None, ["zi"], ["zj"])
         tt(T.zk[:, :], T.zj[:, :], T.b16i[:, :], OP.add, ["zj", "b16i"], ["zk"])
         cp(T.zl[:, :], T.zk[:, :], ["zk"], ["zl"])
         cp(T.X[:, :].indirect(T.zl[:, :]), T.y[:, :], ["y", "zl", "Xp"], ["X"])
         if not last:
+            ts(T.nd[:, :], B[2][:, 384:396], -1.0 / 256, OP.mult, 16.0, OP.add, ["bk2"], ["nd"])
+            empties(256.0)
+            tt(S(7), B[0][:, 192:204], T.nd[:, :], OP.mult, ["bk0", "nd"], ["s7"])
+            tt(S(6), S(1), S(5), OP.max, ["s1", "s5"], ["s6"])
+            tt(S(8), S(7), B[0][:, 256:268], OP.subtract, ["s7", "bk0"], ["s8"])
+            op("V", lambda: g.vector.tensor_reduce(T.aa[:, 0:1], S(8), AxisListType.X, OP.add), ["s8"], ["ar"])
+            mm(B[4][:, 0:1], T.onesf[:, :], T.aa[:, 0:1], True, True, ["onesf", "ar"], ["bk4"])
             ts(T.smi[:, 0:12], T.b37[:, 12 * t + 12:12 * t + 24], B[4][:, 0:1], OP.add, None, None, ["b37", "bk4"], ["fi"])
-            tt(S(2), S(6), S(9), OP.subtract, ["s6", "s9"], ["s2"])
-            tt(S(4), S(1), S(9), OP.add, ["s1", "s9"], ["s4"])
             ts(T.smi[:, 12:24], T.smi[:, 0:12], 2047, OP.bitwise_and, None, None, ["fi"], ["fj"])
-            tt(S(3), S(0), S(2), OP.max, ["s0", "s2"], ["s3"])
-            tt(S(5), S(4), T.smi[:, 12:24], OP.add, ["s4", "fj"], ["s5"])
-            tt(T.cf[:, :], S(3), S(5), OP.max, ["s3", "s5"], ["cf"])
+            tt(S(4), S(9), T.smi[:, 12:24], OP.min, ["s9", "fj"], ["s4"])
+            tt(S(3), S(6), S(4), OP.max, ["s6", "s4"], ["s3"])
+            tt(T.cf[:, :], S(0), S(3), OP.min, ["s0", "s3"], ["cf"])
             cp(T.cl[:, :], T.cf[:, :], ["cf"], ["cl"])
-            ts(T.ai[:, 0:1], B[4][:, 0:1], float(CA), OP.add, None, None, ["bk4"], ["ai0"])
-            ts(T.ai[:, 1:2], T.ai[:, 0:1], 255, OP.bitwise_and, None, None, ["ai0"], ["ai1"])
-            cp(T.aa[:, 1:2], T.ai[:, 1:2], ["ai1"], ["a256"])
+            cp(T.xc[:, :], T.X[:, :].indirect(T.cl[:, :]), ["X", "Xp", "cl"], ["xc"])
+        if t == 0:
+            matrices3()
         act(B[5][:, 0:NP], B[2][:, NP:2 * NP], AF.Identity, ["bk2", "WB"], ["bk5", "wall"], bias=T.WB[:, t:t + 1], scale=-4096.0)
-        ts(T.smi[:, 36:48], T.smi[:, 24:36], 4095, OP.bitwise_and, None, None, ["x2"], ["x3"])
-        ts(T.hoc[:, :], B[2][:, NP:2 * NP], T.SC[:, t:t + 1], OP.add, 16.0, OP.is_equal, ["bk2", "SC"], ["hoc"])
-        cp(T.ql[:, :], T.smi[:, 36:48], ["x3"], ["ql"])
         mm(B[3][:, NP:2 * NP], MB(6), T.oneh[:, :], True, False, ["MB", "oneh"], ["bk3"])
         mm(B[3][:, NP:2 * NP], MB(1), T.K1[:, :], False, False, ["MB", "K1"], ["bk3"])
-        for c in range(2):
-            windows(t, c)
-        mm(B[3][:, NP:2 * NP], T.I8n[:, :], T.hoc[:, :], False, True, ["I8n", "hoc"], ["bk3"])
-        for c in range(2, 8 if last else 6):
-            windows(t, c)
-        tt(T.C1[:, :], B[3][:, NP:2 * NP], T.crep[:, :], OP.max, ["bk3", "crep"], ["C1"])
-        tt(B[5][:, NP:2 * NP], T.C1[:, :], T.Hp[:, :], OP.min, ["C1", "Hp"], ["bk5", "R3p"])
 
     dma("S", "ox", T.yx[:, :], T.X[:, 0:3072], ["X"], [])
+    lists()
+    turn2(V - 1)
+    card_c(V - 1)
+    turned()
     ts(T.oya[:, :], T.Tc[:, :], 1536.0, OP.add, None, None, ["Tc"], ["oya"])
     ts(T.IH[:, 0:NP], T.Tc[:, :], EMPTY, OP.is_lt, None, None, ["Tc"], ["inv"])
     tt(T.oyt[:, :], T.oya[:, :], T.IH[:, 0:NP], OP.mult, ["oya", "inv"], ["oyt"])
     dma("S", "ot", T.yt[:, :], T.oyt[:, :], ["oyt"], [])
-    turned()
+    card_c2(V - 1)
+    tt(B[5][:, NP:2 * NP], B[5][:, NP:2 * NP], T.Hp[:, :], OP.min, ["C1", "bk5", "Hp"], ["bk5", "R3p"])
     hand_end()
     ts(T.IH[:, NP:2 * NP], T.Hs[:, :], EMPTY, OP.is_lt, None, None, ["Hs"], ["hinv"])
     mm(B[1][:, 0:NP], T.UR[:, :], T.Hs[:, :], True, True, ["UR", "Hs"], ["bk1"])

from concourse.mybir import AluOpType, AxisListType, ActivationFunctionType

OP = AluOpType
AF = ActivationFunctionType
V = 6
NP = 192
CW = 3088
EMPTY = 1536.0
PARTS = ("MX", "cols", "b", "RW", "RA", "WIN", "WINA", "MB")
CA = 8 * 16 * (191 * 192 // 2)
RND = 8388608.0

SCRATCH = {
    "X": ("sbuf", [128, CW], "bfloat16"),
    "XT": ("sbuf", [128, 3072], "bfloat16"),
    "MX": ("sbuf", [128, 3072], "bfloat16"),
    "IOT": ("sbuf", [128, 3072], "float32"),
    "WIN": ("sbuf", [128, 4096], "float32"),
    "WINA": ("sbuf", [128, 1024], "float32"),
    "RW": ("sbuf", [128, 16 * 128], "float16"), "RA": ("sbuf", [128, 4 * 128], "float16"), "Tg": ("sbuf", [128, NP], "float16"),
    "qm": ("sbuf", [128, 12], "uint16"),
    "nmi": ("sbuf", [8, 576], "int32"), "nmf": ("sbuf", [8, 576], "float32"), "R8": ("sbuf", [8, 128], "float32"),
    "tri": ("sbuf", [128, NP], "int32"), "hai": ("sbuf", [128, NP], "int32"), "wti": ("sbuf", [128, 1], "int32"),
    "smB": ("sbuf", [128, 272], "bfloat16"), "smC": ("sbuf", [128, 256], "bfloat16"), "smA": ("sbuf", [128, 256], "bfloat16"),
    "cwi": ("sbuf", [128, 16], "int32"), "cwj": ("sbuf", [128, 16], "int32"), "cw": ("sbuf", [128, 16], "float32"),
    "SC": ("sbuf", [128, 16], "float32"), "E0": ("sbuf", [128, 16], "float32"), "PC": ("sbuf", [128, 16], "float32"),
    "WB": ("sbuf", [128, 16], "float32"), "cols": ("sbuf", [128, 16], "float32"),
    "iq": ("sbuf", [128, 12], "float32"), "bi": ("sbuf", [128, 12], "float32"), "b16i": ("sbuf", [128, 12], "int32"),
    "b16h": ("sbuf", [128, 12], "float16"), "b37": ("sbuf", [128, 12 * V], "float32"),
    "onesf": ("sbuf", [128, 128], "float32"), "ones": ("sbuf", [128, NP], "bfloat16"), "oneh": ("sbuf", [128, NP], "float16"),
    "Ib": ("sbuf", [128, 128], "bfloat16"), "NB": ("sbuf", [128, 128], "bfloat16"),
    "W2": ("sbuf", [128, 144], "bfloat16"), "WN": ("sbuf", [128, 144], "bfloat16"), "Ww": ("sbuf", [128, 144], "bfloat16"),
    "Wk": ("sbuf", [128, 144], "float16"), "W0": ("sbuf", [128, 144], "float16"), "W256": ("sbuf", [128, 144], "float16"),
    "Ih": ("sbuf", [128, 256], "float16"), "SI": ("sbuf", [128, 256], "float16"), "E15": ("sbuf", [128, 256], "float16"),
    "IN": ("sbuf", [128, 256], "float16"), "TUr": ("sbuf", [128, 256], "float16"), "BA": ("sbuf", [128, 128], "float16"),
    "BH": ("sbuf", [128, 256], "float16"), "TUi": ("sbuf", [128, 128], "float16"), "TU8": ("sbuf", [128, 128], "float16"),
    "I8": ("sbuf", [128, 128], "float16"), "I8n": ("sbuf", [128, 128], "float16"), "MB": ("sbuf", [128, 8 * 128], "float16"),
    "M8": ("sbuf", [128, 8], "float16"), "UR": ("sbuf", [128, 128], "float16"),
    "thr": ("sbuf", [128, NP], "float32"), "lim": ("sbuf", [128, NP], "float32"),
    "Th": ("sbuf", [128, NP], "float16"), "IH": ("sbuf", [128, 3 * NP], "float16"), "Hs": ("sbuf", [128, NP], "float16"),
    "Hp": ("sbuf", [128, NP], "float16"), "ff": ("sbuf", [128, NP], "float16"), "oh": ("sbuf", [128, NP], "float16"),
    "fT": ("sbuf", [128, NP], "float16"), "ohc": ("sbuf", [128, NP], "float16"), "crep0": ("sbuf", [128, NP], "float32"),
    "crep1": ("sbuf", [128, NP], "float32"),
    "Trot": ("sbuf", [128, NP], "float32"), "xc": ("sbuf", [128, NP], "bfloat16"), "na": ("sbuf", [128, NP], "bfloat16"),
    "ok": ("sbuf", [128, NP], "float16"), "K1": ("sbuf", [128, NP], "float16"), "fst": ("sbuf", [128, NP], "float16"),
    "Tc": ("sbuf", [128, NP], "float16"), "ac": ("sbuf", [128, NP], "float32"), "vv": ("sbuf", [128, NP], "float32"),
    "uu": ("sbuf", [128, NP], "float32"), "au": ("sbuf", [128, NP], "float32"), "y": ("sbuf", [128, NP], "bfloat16"),
    "Tcap": ("sbuf", [128, NP], "float16"), "hoc": ("sbuf", [128, NP], "float16"),
    "Rv": ("sbuf", [128, NP], "float32"), "R2": ("sbuf", [128, NP], "float32"),
    "cf": ("sbuf", [128, 12], "float32"), "cl": ("sbuf", [128, 12], "uint16"), "kl": ("sbuf", [128, 12], "uint16"),
    "zl": ("sbuf", [128, 12], "uint16"), "ql": ("sbuf", [128, 12], "uint16"),
    "zi": ("sbuf", [128, 12], "int32"), "zj": ("sbuf", [128, 12], "int32"), "zk": ("sbuf", [128, 12], "int32"),
    "x1": ("sbuf", [128, 12], "float32"), "nd": ("sbuf", [128, 12], "float32"),
    "sm": ("sbuf", [128, 12 * 10], "float32"), "smi": ("sbuf", [128, 12 * 5], "int32"),
    "aa": ("sbuf", [128, 4], "float32"), "ai": ("sbuf", [128, 2], "int32"),
    "oyh": ("sbuf", [128, NP], "float32"), "oyt": ("sbuf", [128, NP], "float32"), "oya": ("sbuf", [128, NP], "float32"),
    "oyb": ("sbuf", [128, NP], "float32"), "omn": ("sbuf", [8, 2 * NP], "float32"),
}
for _i in range(8):
    SCRATCH["bk%d" % _i] = ("psum", [128, 512], "float32")
for _i in range(V):
    SCRATCH["TT%d" % _i] = ("sbuf", [128, NP], "uint16")
for _i in range(V - 1):
    SCRATCH["TO%d" % _i] = ("sbuf", [128, NP], "uint16")

DMAS = ["dx", "dt", "dh", "dn", "dm", "dth", "dw", "ox", "oh", "ot", "om", "on"]
SEMAPHORES = ["qV", "qA", "qP", "qG", "snd"] + ["arr%d" % i for i in range(1, V)] + ["d_" + n for n in DMAS]


def send_engines(topo, src, dst):
    return topo.engines(src, dst)[:8]


def rank_program(g, core, T, topo):
    rank = T.rank_of(core)
    if rank is None:
        return
    ops = []
    writer, readers, bank = {}, {}, {}

    def op(q, f, r=(), w=(), dma=None):
        k = len(ops)
        deps = set()
        for n in r:
            if n[:2] == "bk":
                continue
            if n in writer:
                deps.add(writer[n])
            readers.setdefault(n, []).append(k)
        for n in w:
            if n[:2] == "bk":
                continue
            if n in writer and (ops[writer[n]]["q"] != q or ops[writer[n]]["dma"] or n.rstrip("0123456789_") not in PARTS):
                deps.add(writer[n])
            for i in readers.get(n, []):
                if i != k:
                    deps.add(i)
            writer[n] = k
            readers[n] = []
        for n in list(r) + list(w):
            if n[:2] == "bk":
                a = bank.setdefault(n, {})
                for q2 in a:
                    if q2 != q:
                        deps.add(a[q2])
                a[q] = k
        ops.append({"q": q, "f": f, "deps": deps, "dma": dma})
        return k

    def ts(out, in0, s1, o1, s2, o2, r, w):
        if o2 is None:
            op("V", lambda: g.vector.tensor_scalar(out, in0, s1, None, o1), r, w)
        else:
            op("V", lambda: g.vector.tensor_scalar(out, in0, s1, s2, o1, o2), r, w)

    def tt(out, a, b, o, r, w):
        op("V", lambda: g.vector.tensor_tensor(out, a, b, o), r, w)

    def cp(out, a, r, w):
        op("V", lambda: g.vector.tensor_copy(out, a), r, w)

    def act(out, a, fn, r, w, bias=0.0, scale=1.0):
        op("A", lambda: g.scalar.activation(out, a, fn, bias=bias, scale=scale), r, w)

    def mm(out, l, rr, st, sp, r, w):
        op("P", lambda: g.tensor.matmul(out, l, rr, st, sp), r, w)

    def dma(q, name, out, in_, r, w):
        e = {"S": g.sync, "A": g.scalar}[q]
        op(q, lambda: e.dma_start(out, in_), r, w, dma="d_" + name)

    def ms(ap, c, w):
        op("V", lambda: g.vector.memset(ap, c), [], [w])

    def MB(j):
        return T.MB[:, 128 * j:128 * j + 128]

    def S(j):
        return T.sm[:, 12 * j:12 * j + 12]

    def diag(o, mat, src, so, n, r, wb, first=True):
        for j in range(16):
            mm(o, T[mat][:, 16 - j:144 - j], T[src][:, so + j:so + NP * n:16], first and j == 0, j == 15, r + [mat], [wb])

    B = [T["bk%d" % i] for i in range(8)]
    SP = T.SC[:, 15:16]

    dma("S", "dm", T.nmi[:, NP:2 * NP], T.mh[:, :], [], ["nmi_m"])
    dma("A", "dh", T.hai[:, :], T.hands[:, :], [], ["hai"])
    dma("S", "dn", T.nmi[:, 0:NP], T.nt[:, :], [], ["nmi_n"])
    dma("A", "dx", T.X[:, 0:3072], T.x0[:, :], [], ["X"])
    dma("S", "dt", T.tri[:, :], T.trains[:, :], [], ["tri"])
    dma("S", "dth", T.nmi[:, 2 * NP:3 * NP], T.th[:, :], [], ["nmi_t"])
    dma("S", "dw", T.wti[:, :], T.wt[:, :], [], ["wti"])

    blk = [[0, 2], [-16, 8], [0, 16]]
    blk2 = [[0, 2], [16, 8], [0, 16]]
    op("G", lambda: g.iota(T.cwi[:, :], [[1, 16]], 128, -1), [], ["cwi"])
    op("G", lambda: g.iota(T.smA[:, :], [[0, 16], [1, 16]], 0, 0, allow_small_or_imprecise_dtypes=True), [], ["smA"])
    ms(T.R8[:, :], 1.0, "R8")
    ms(T.smB[:, 0:16], -99.0, "smBp")
    ms(T.X[:, 3072:CW], 0.0, "Xp")
    ms(T.onesf[:, :], 1.0, "onesf")
    ms(T.ones[:, :], 1.0, "ones")
    for b in (6, 7):
        ms(B[b][:, 192:256], 0.0, "bk%d" % b)

    def blocks(nm, fill, o):
        op("G", lambda: g.affine_select(T[nm][:, o:o + 256], T.smA[:, :], blk, OP.is_ge, fill, 0, 1), ["smA"], [nm])
        op("G", lambda: g.affine_select(T[nm][:, o:o + 256], T[nm][:, o:o + 256], blk2, OP.is_ge, fill, 15, -1), [nm], [nm])

    blocks("smB", -99.0, 16)
    op("G", lambda: g.affine_select(T.R8[:, :], T.R8[:, :], [[1, 128]], OP.is_ge, 0.0, 0, -16), ["R8"], ["R8"])
    op("G", lambda: g.affine_select(T.R8[:, :], T.R8[:, :], [[-1, 128]], OP.is_ge, 0.0, 15, 16), ["R8"], ["R8"])
    op("G", lambda: g.iota(T.iq[:, :], [[16, 12]], 0, 0, allow_small_or_imprecise_dtypes=True), [], ["iq"])
    blocks("smC", 99.0, 0)
    op("G", lambda: g.iota(T.IOT[:, :], [[1, 3072]], -1536, 0, allow_small_or_imprecise_dtypes=True), [], ["IOT"])

    smb = T.smB[:, 16:144]
    smb2 = T.smB[:, 16:272]
    smp = T.smB[:, 0:144]
    ts(T.cwj[:, :], T.cwi[:, :], 15, OP.bitwise_and, None, None, ["cwi"], ["cwj"])
    cp(T.cw[:, :], T.cwj[:, :], ["cwj"], ["cw"])
    ts(T.SC[:, :], T.cw[:, :], -1.0, OP.mult, 15.0, OP.add, ["cw"], ["SC"])
    ts(T.E0[:, :], T.cw[:, :], 0.0, OP.is_equal, None, None, ["cw"], ["E0"])
    ts(T.cols[:, 0:1], SP, 1.0, OP.is_ge, None, None, ["SC"], ["cols"])
    ts(T.cols[:, 1:2], SP, -1.0, OP.add, None, None, ["SC"], ["cols"])
    ts(T.cols[:, 2:3], SP, -1.0, OP.mult, 16.0, OP.add, ["SC"], ["cols"])
    row0 = (1536.0, -4096.0, 512.0, -1025.0 / 2048, 1.0, 2048.0, 6144.0, -512.0)
    for j, v in enumerate(row0):
        ts(T.cols[:, 3 + j:4 + j], T.E0[:, 0:1], v, OP.mult, None, None, ["E0"], ["cols"])
    ts(T.PC[:, :], T.E0[:, :], 5632.0, OP.mult, -4096.0, OP.add, ["E0"], ["PC"])
    ts(T.WB[:, :], T.SC[:, :], -4096.0, OP.mult, 4096.0 * 16.5, OP.add, ["SC"], ["WB"])
    ts(T.W0[:, :], smp, 0.0, OP.is_equal, T.E0[:, 0:1], OP.mult, ["smB", "smBp", "E0"], ["W0"])

    ts(T.Ib[:, :], smb, SP, OP.is_equal, None, None, ["smB", "SC"], ["Ib"])
    ts(T.NB[:, :], smb, 0.0, OP.is_ge, -1.0, OP.mult, ["smB"], ["NB"])
    ts(T.W2[:, :], smp, 0.0, OP.is_equal, 2.0, OP.mult, ["smB", "smBp"], ["W2"])
    ts(T.WN[:, :], smp, 0.0, OP.is_equal, -1.0, OP.mult, ["smB", "smBp"], ["WN"])
    ts(T.BA[:, :], smb, 0.0, OP.is_ge, None, None, ["smB"], ["BA"])
    ts(T.I8[:, :], smb, SP, OP.is_equal, 8192.0, OP.mult, ["smB", "SC"], ["I8"])
    ts(T.Ih[:, :], smb2, SP, OP.is_equal, None, None, ["smB", "SC"], ["Ih"])

    def spread(j, nm, b):
        cp(T.nmf[:, NP * j:NP * j + NP], T.nmi[:, NP * j:NP * j + NP], [nm], [nm + "f"])
        mm(B[b][:, 0:NP], T.R8[:, :], T.nmf[:, NP * j:NP * j + NP], True, True, ["R8", nm + "f"], ["bk%d" % b])

    spread(1, "nmi_m", 4)
    ts(T.bi[:, :], T.iq[:, :], SP, OP.add, None, None, ["iq", "SC"], ["bi"])
    ts(T.b37[:, 0:12], T.bi[:, :], 37.0, OP.mult, None, None, ["bi"], ["b37"])
    ts(T.oyt[:, :], B[4][:, 0:NP], SP, OP.is_le, 3072.0, OP.mult, ["bk4", "SC"], ["tb"])
    tt(T.oyb[:, :], T.oyt[:, :], T.hai[:, :], OP.max, ["tb", "hai"], ["h0f"])
    ts(T.Hs[:, :], T.oyb[:, :], -1536.0, OP.add, None, None, ["h0f"], ["Hs"])
    diag(B[2][:, 408:420], "W0", "Hs", 0, 1, ["Hs"], "bk2")
    spread(0, "nmi_n", 5)
    ts(T.oyh[:, :], B[5][:, 0:NP], SP, OP.is_le, 3072.0, OP.mult, ["bk5", "SC"], ["ta"])
    tt(T.oya[:, :], T.oyh[:, :], T.tri[:, :], OP.max, ["ta", "tri"], ["t0f"])
    cp(T.TT0[:, :], T.oya[:, :], ["t0f"], ["TT0"])

    def empties(scale):
        pd = B[2][:, 408:420]
        ts(S(1), pd, EMPTY * scale, OP.is_lt, 4096.0, OP.mult, ["bk2"], ["s1"])
        ts(S(0), pd, 1.0 / scale, OP.mult, 1536.0, OP.add, ["bk2"], ["s0"])

    empties(1.0)
    cp(T.smi[:, 0:12], T.b37[:, 0:12], ["b37"], ["fi"])
    ts(T.smi[:, 12:24], T.smi[:, 0:12], 2047, OP.bitwise_and, None, None, ["fi"], ["fj"])
    tt(S(4), S(1), T.smi[:, 12:24], OP.max, ["fj", "s1"], ["s4"])
    tt(T.cf[:, :], S(0), S(4), OP.min, ["s0", "s4"], ["cf"])
    cp(T.cl[:, :], T.cf[:, :], ["cf"], ["cl"])

    def matrices():
        ts(T.SI[:, :], smb2, T.cols[:, 1:2], OP.is_equal, None, None, ["smB", "cols"], ["SI"])
        ts(T.E15[:, :], smb2, 15.0, OP.is_equal, T.cols[:, 3:4], OP.mult, ["smB", "cols"], ["E15"])
        tt(T.SI[:, :], T.SI[:, :], T.Ih[:, :], OP.subtract, ["SI", "Ih"], ["SI"])
        ts(T.IN[:, :], smb2, SP, OP.is_equal, -1536.0, OP.mult, ["smB", "SC"], ["IN"])
        ts(T.TUr[:, :], T.smC[:, :], SP, OP.is_lt, -4096.0, OP.mult, ["smC", "SC"], ["TUr"])
        ts(T.TUi[:, :], T.smC[:, 0:128], SP, OP.is_le, None, None, ["smC", "SC"], ["TUi"])
        ts(T.TU8[:, :], T.smC[:, 0:128], SP, OP.is_lt, 4096.0, OP.mult, ["smC", "SC"], ["TU8"])
        ts(T.BH[:, :], smb2, 0.0, OP.is_ge, 8192.0, OP.mult, ["smB"], ["BH"])
        for j in range(len(row0)):
            ts(MB(j), smb, 0.0, OP.is_ge, T.cols[:, 3 + j:4 + j], OP.mult, ["smB", "cols"], ["MB"])
        for t in range(1, V):
            ts(T.b37[:, 12 * t:12 * t + 12], T.bi[:, :], 37.0, OP.mult, float(613 * t + CA), OP.add, ["bi"], ["b37"])
        ts(T.b16h[:, :], T.bi[:, :], 16.0, OP.mult, None, None, ["bi"], ["b16h"])
        ts(T.Wk[:, :], smp, 0.0, OP.is_equal, T.cols[:, 0:1], OP.mult, ["smB", "smBp", "cols"], ["Wk"])
        ts(T.W256[:, :], smp, 0.0, OP.is_equal, 256.0, OP.mult, ["smB", "smBp"], ["W256"])
        cp(T.oneh[:, :], T.ones[:, :], ["ones"], ["oneh"])

    def matrices2():
        cp(T.cols[:, 12:13], T.wti[:, :], ["wti"], ["wtf"])
        ts(T.b16i[:, :], T.bi[:, :], 16.0, OP.mult, None, None, ["bi"], ["b16i"])
        ts(T.I8n[:, :], smb, SP, OP.is_equal, -4096.0, OP.mult, ["smB", "SC"], ["I8n"])
        ts(T.Ww[:, :], smp, 0.0, OP.is_equal, T.cols[:, 12:13], OP.mult, ["smB", "smBp", "wtf"], ["Ww"])

        for w in range(4):
            ts(T.RA[:, 128 * w:128 * w + 128], smb, T.SC[:, 15 - w:16 - w], OP.is_equal, None, None, ["smB", "SC"], ["RA"])

    def matrices3():
        for w in range(16):
            ts(T.RW[:, 128 * w:128 * w + 128], smb, T.cw[:, w:w + 1], OP.is_equal, None, None, ["smB", "cw"], ["RW"])
        ts(T.M8[:, :], T.smB[:, 16:144:16], 0.0, OP.is_ge, None, None, ["smB"], ["M8"])
        ts(T.UR[:, :], smb, T.SC[:, V - 1:V], OP.is_equal, None, None, ["smB", "SC"], ["UR"])


    def turn1():
        for c in range(2):
            for h in range(2):
                w = 2 * c + h
                mm(B[6 + c][:, 256 * h:256 * h + NP], T.RA[:, 128 * w:128 * w + 128], T.Tcap[:, :], True, True, ["RA", "Tcap"], ["bk%d" % (6 + c)])
            act(T.WINA[:, 512 * c:512 * c + 448], B[6 + c][:, 0:448], AF.Copy, ["bk%d" % (6 + c)], ["WINA"])

    def turn2(t):
        cp(T.Tg[:, :], T.WINA[:, :].indirect(T.ql[:, :]), ["WINA", "ql"], ["Tg"])
        for c in range(2):
            for h in range(2):
                w = (t + 1 - 4 * (2 * c + h)) % 16
                mm(B[6 + c][:, 256 * h:256 * h + NP], T.RW[:, 128 * w:128 * w + 128], T.Tg[:, :], True, True, ["RW", "Tg"], ["bk%d" % (6 + c)])

    def turned():
        for c in range(2):
            for h in range(2):
                o = 1024 * (2 * c + h)
                act(T.WIN[:, o:o + NP], B[6 + c][:, 256 * h:256 * h + NP], AF.Copy, ["bk%d" % (6 + c)], ["WIN"])
        act(T.Rv[:, :], T.WIN[:, :].indirect(T.qm[:, :]), AF.Copy, ["WIN", "qm"], ["Rv"])

    def lists():
        tt(T.x1[:, :], B[2][:, 384:396], T.bi[:, :], OP.add, ["bk2", "bi"], ["x1"])
        tt(T.smi[:, 24:36], B[2][:, 396:408], T.x1[:, :], OP.add, ["bk2", "x1"], ["x2"])
        ts(T.smi[:, 36:48], T.smi[:, 24:36], 1023, OP.bitwise_and, None, None, ["x2"], ["x3"])
        ts(T.smi[:, 48:60], T.smi[:, 24:36], 3072 + 255, OP.bitwise_and, None, None, ["x2"], ["x4"])
        cp(T.ql[:, :], T.smi[:, 36:48], ["x3"], ["ql"])
        cp(T.qm[:, :], T.smi[:, 48:60], ["x4"], ["qm"])

    def card_c(t):
        ts(T.hoc[:, :], B[2][:, NP:2 * NP], T.SC[:, t:t + 1], OP.add, 16.0, OP.is_equal, ["bk2", "SC"], ["hoc"])
        mm(B[3][:, NP:2 * NP], T.I8n[:, :], T.hoc[:, :], False, True, ["I8n", "hoc"], ["bk3"])

    def card_c2(t):
        tt(B[5][:, NP:2 * NP], B[3][:, NP:2 * NP], T["crep%d" % (t % 2)][:, :], OP.max, ["bk3", "crep%d" % (t % 2)], ["bk5", "C1"])

    def hand_end():
        tt(T.R2[:, :], B[5][:, 0:NP], T.Rv[:, :], OP.max, ["Rv", "bk5", "wall"], ["R2"])
        tt(T.Hs[:, :], B[5][:, NP:2 * NP], T.R2[:, :], OP.min, ["R2", "bk5", "R3p"], ["Hs"])

    def hand_begin(t):
        ts(T.Hp[:, :], T.Hs[:, :], T.PC[:, t:t + 1], OP.max, None, None, ["Hs", "PC"], ["Hp"])
        ts(T.IH[:, NP:2 * NP], T.Hp[:, :], EMPTY, OP.is_ge, None, None, ["Hp"], ["hinv"])
        if t < V - 1:
            ts(T.IH[:, 2 * NP:3 * NP], T.Hp[:, :], T.E0[:, t + 1:t + 2], OP.mult, None, None, ["Hp", "E0"], ["hfr"])

    cp(T.xc[:, :], T.X[:, :].indirect(T.cl[:, :]), ["X", "Xp", "cl"], ["xc"])
    for t in range(V):
        last = t == V - 1
        tn = "TT%d" % t
        tab = T[tn]
        jj = 0 if last else (2 if t == 3 else 1)
        ro = 128 - 16 * jj

        def rot(nm):
            return T[nm][:, ro:ro + 128] if jj else T[nm][:, 0:128]

        def chunk(c):
            for s in range(4):
                o = 256 * (c % 2)
                tt(T.MX[:, 1024 * c + s:1024 * c + 1024:4], B[1][:, o:o + 256], T.XT[:, 1024 * c + s:1024 * c + 1024:4], OP.max,
                   ["bk1", "XT%d" % c], ["MX%d_%d" % (c, s)])

        def fours(c, n):
            for s in range(4):
                mm(B[1][:, s:256 * n:4], T.Ib[:, :], T.xc[:, 64 * c:64 * c + 64 * n], True, True, ["Ib", "xc"], ["bk1"])

        def sumx(c):
            for s in range(16):
                mm(B[0][:, 64 * c:64 * c + 64], T.WN[:, 16 - s:144 - s], T.XT[:, 1024 * c + s:1024 * c + 1024:16], False, False, ["WN", "XT%d" % c], ["bk0"])

        def summ(c):
            for k in range(16):
                s = k // 4 + 4 * (k % 4)
                mm(B[0][:, 64 * c:64 * c + 64], T.W2[:, 16 - s:144 - s], T.MX[:, 1024 * c + s:1024 * c + 1024:16], False, c == 2 and k == 15,
                   ["W2", "MX%d_%d" % (c, s % 4)], ["bk0"])

        if t > 0:
            op("R", None, [], [tn], dma="arr%d" % t)
        cp(T.xc[:, :], T.X[:, :].indirect(T.cl[:, :]), ["X", "Xp", "cl"], ["xc"])
        def gather(c):
            act(T.XT[:, 1024 * c:1024 * c + 1024], T.X[:, :].indirect(tab[:, 64 * c:64 * c + 64]), AF.Copy, ["X", "Xp", tn], ["XT%d" % c])

        crn = "crep%d" % (t % 2)
        fours(0, 2)
        mm(B[0][:, 0:NP], T.NB[:, :], T.xc[:, :], True, False, ["NB", "xc"], ["bk0"])
        if t > 0:
            lists()
            ts(T.ai[:, 0:1], B[4][:, 0:1], float(CA), OP.add, None, None, ["bk4"], ["ai0"])
            ts(T.ai[:, 1:2], T.ai[:, 0:1], 255, OP.bitwise_and, None, None, ["ai0"], ["ai1"])
            cp(T.aa[:, 1:2], T.ai[:, 1:2], ["ai1"], ["a256"])
            card_c(t - 1)
        ts(T.Th[:, :], tab[:, :], -1536.0, OP.add, None, None, [tn], ["Th"])
        ts(T.IH[:, 0:NP], tab[:, :], 3072.0, OP.is_ge, None, None, [tn], ["inv"])
        ts(T.na[:, :], T.xc[:, :], -1.0, OP.mult, None, None, ["xc"], ["na"])
        gather(0)
        mm(B[2][:, 0:NP], T.BA[:, :], T.IH[:, 0:NP], True, True, ["BA", "inv"], ["bk2"])
        mm(B[4][:, 0:NP], rot("Ih"), T.Th[:, :], True, True, ["Ih", "Th"], ["bk4"])
        mm(B[0][:, 0:NP], T.I8[:, :], T.IH[:, 0:NP], False, False, ["I8", "inv"], ["bk0"])
        sumx(0)
        chunk(0)
        summ(0)
        if t == 0:
            spread(2, "nmi_t", 6)
            matrices()
            matrices2()
        gather(1)
        act(T.Trot[:, :], B[4][:, 0:NP], AF.Copy, ["bk4"], ["Trot"])
        act(T[crn][:, :], T.IOT[:, :].indirect(T.cl[:, :]), AF.Copy, ["IOT", "cl"], [crn])
        gather(2)
        if t == 0:
            act(T.thr[:, :], B[6][:, 0:NP], AF.Copy, ["bk6"], ["thr"])
            act(T.lim[:, :], T.thr[:, :], AF.Copy, ["thr"], ["lim"])
        else:
            act(T.lim[:, :], T.thr[:, :], AF.Identity, ["thr", "a256"], ["lim"], bias=T.aa[:, 1:2])
        if t > 0:
            card_c2(t - 1)
            tt(B[5][:, NP:2 * NP], B[5][:, NP:2 * NP], T.Hp[:, :], OP.min, ["C1", "bk5", "Hp"], ["bk5", "R3p"])
        mm(B[7][:, 0:NP], T.Ih[:, 0:128], T.Th[:, :], True, True, ["Ih", "Th"], ["bk7"])
        sumx(1)
        ts(T.ff[:, :], B[2][:, 0:NP], 0.0, OP.is_equal, None, None, ["bk2"], ["ff"])
        ts(T.oh[:, :], B[2][:, 0:NP], 1.0, OP.max, T.cols[:, 2:3], OP.is_equal, ["bk2", "cols"], ["oh"])
        tt(T.fT[:, :], B[7][:, 0:NP], T.ff[:, :], OP.mult, ["ff", "bk7"], ["fT"])
        pt = B[3][:, 0:NP]
        mm(pt, rot("Ih"), T.Th[:, :], True, False, ["Ih", "Th"], ["bk3"])
        mm(pt, rot("E15"), T.ff[:, :], False, False, ["E15", "ff"], ["bk3"])
        mm(pt, rot("IN"), T.oh[:, :], False, False, ["IN", "oh"], ["bk3"])
        mm(pt, rot("SI"), T.fT[:, :], False, False, ["SI", "fT"], ["bk3"])
        mm(B[2][:, 0:NP], MB(0), T.oneh[:, :], True, False, ["MB", "oneh"], ["bk2"])
        pac = B[4][:, NP:2 * NP]
        mm(pac, T.Ib[:, :], T.xc[:, :], True, False, ["Ib", "xc"], ["bk4"])
        mm(pac, MB(7), T.oneh[:, :], False, False, ["MB", "oneh"], ["bk4"])
        if t > 0:
            turn2(t - 1)
        chunk(1)
        summ(1)
        fours(2, 1)
        if t > 0:
            turned()
        tt(T.ohc[:, :], T.oh[:, :], T[crn][:, :], OP.mult, ["oh", crn], ["ohc"])
        sumx(2)
        mm(pt, rot("Ih"), T.ohc[:, :], False, False, ["Ih", "ohc"], ["bk3"])
        chunk(2)
        summ(2)

        tt(T.ok[:, :], B[0][:, 0:NP], T.lim[:, :], OP.is_le, ["bk0", "lim"], ["ok"])
        mm(B[1][:, 0:NP], T.TUi[:, :], T.ok[:, :], True, True, ["TUi", "ok"], ["bk1"])
        mm(B[2][:, 0:NP], rot("TUr"), T.ok[:, :], False, True, ["TUr", "ok"], ["bk2"])
        mm(pt, rot("BH"), T.ok[:, :], False, True, ["BH", "ok"], ["bk3"])
        mm(B[0][:, 256:268], T.Ih[:, 0:128], T.b16h[:, :], True, False, ["Ih", "b16h"], ["bk0"])
        ts(T.K1[:, :], B[1][:, 0:NP], 0.5, OP.is_ge, None, None, ["bk1"], ["K1"])
        mm(pac, MB(2), T.K1[:, :], False, True, ["MB", "K1"], ["bk4"])
        diag(B[0][:, 256:268], "Wk", "K1", 0, 1, ["K1"], "bk0", first=False)
        tt(T.fst[:, :], B[2][:, 0:NP], T.Trot[:, :], OP.max, ["bk2", "Trot"], ["fst"])
        tt(T.Tc[:, :], B[3][:, 0:NP], T.fst[:, :], OP.min, ["bk3", "fst"], ["Tc"])
        if not last:
            to = T["TO%d" % t]
            nxt = T.cores[(rank + 1) % len(T.cores)]
            ts(to[:, :], T.Tc[:, :], 1536.0, OP.add, None, None, ["Tc"], ["TO%d" % t])
            rid, pid = topo.addr(nxt, core)
            mask = 0
            for e in send_engines(topo, core, nxt):
                mask |= 1 << e
            op("G", lambda to=to, t=t, rid=rid, pid=pid, mask=mask: g.remote_dma(T["TT%d" % (t + 1)][:, :], to[:, :], T.sem["arr%d" % (t + 1)], T.sem.snd, pid, rid, mask),
               ["TO%d" % t], [], dma="snd")
        mm(B[1][:, NP:2 * NP], MB(4), T.oneh[:, :], True, False, ["MB", "oneh"], ["bk1"])
        mm(B[1][:, NP:2 * NP], MB(3), T.K1[:, :], False, True, ["MB", "K1"], ["bk1"])
        mm(B[3][:, 0:NP], MB(5), T.oneh[:, :], True, False, ["MB", "oneh"], ["bk3"])
        mm(B[3][:, 0:NP], T.TU8[:, :], T.ok[:, :], False, False, ["TU8", "ok"], ["bk3"])
        mm(B[3][:, 0:NP], MB(1), T.K1[:, :], False, True, ["MB", "K1"], ["bk3"])
        tt(T.ac[:, :], B[4][:, NP:2 * NP], T.na[:, :], OP.max, ["bk4", "na"], ["ac"])
        if t > 0:
            hand_end()
        cp(T.kl[:, :], B[0][:, 256:268], ["bk0"], ["kl"])
        tt(T.vv[:, :], T.XT[:, :].indirect(T.kl[:, :]), T.ac[:, :], OP.add, ["XT0", "XT1", "XT2", "kl", "ac"], ["vv"])
        tt(T.uu[:, :], B[1][:, NP:2 * NP], T.vv[:, :], OP.mult, ["bk1", "vv"], ["uu"])
        act(T.au[:, :], T.uu[:, :], AF.Abs, ["uu"], ["au"])
        tt(T.Tcap[:, :], B[3][:, 0:NP], T.Th[:, :], OP.max, ["bk3", "Th"], ["Tcap"])
        if not last:
            diag(B[0][:, 192:204], "W0", "K1", 0, 1, ["K1"], "bk0")
        turn1()
        ts(T.y[:, :], T.au[:, :], RND, OP.add, -RND, OP.add, ["au"], ["y"])
        diag(B[1][:, 0:12], "Ww", "y", 0, 1, ["y"], "bk1")
        hand_begin(t)
        mm(B[2][:, NP:2 * NP], T.BA[:, :], T.IH[:, NP:2 * NP], True, True, ["BA", "hinv"], ["bk2"])
        diag(B[2][:, 384:408 if last else 420], "W256", "IH", 0, 2 if last else 3, ["inv", "hinv", "hfr"], "bk2")
        if not last:
            tt(S(5), B[0][:, 192:204], T.cf[:, :], OP.mult, ["bk0", "cf"], ["s5"])
            ts(S(9), B[0][:, 192:204], -4096.0, OP.mult, 4096.0, OP.add, ["bk0"], ["s9"])
        cp(T.zi[:, :], B[1][:, 0:12], ["bk1"], ["zi"])
        ts(T.zj[:, :], T.zi[:, :], 15, OP.bitwise_and, None, None, ["zi"], ["zj"])
        tt(T.zk[:, :], T.zj[:, :], T.b16i[:, :], OP.add, ["zj", "b16i"], ["zk"])
        cp(T.zl[:, :], T.zk[:, :], ["zk"], ["zl"])
        cp(T.X[:, :].indirect(T.zl[:, :]), T.y[:, :], ["y", "zl", "Xp"], ["X"])
        if not last:
            ts(T.nd[:, :], B[2][:, 384:396], -1.0 / 256, OP.mult, 16.0, OP.add, ["bk2"], ["nd"])
            empties(256.0)
            tt(S(7), B[0][:, 192:204], T.nd[:, :], OP.mult, ["bk0", "nd"], ["s7"])
            tt(S(6), S(1), S(5), OP.max, ["s1", "s5"], ["s6"])
            tt(S(8), S(7), B[0][:, 256:268], OP.subtract, ["s7", "bk0"], ["s8"])
            op("V", lambda: g.vector.tensor_reduce(T.aa[:, 0:1], S(8), AxisListType.X, OP.add), ["s8"], ["ar"])
            mm(B[4][:, 0:1], T.onesf[:, :], T.aa[:, 0:1], True, True, ["onesf", "ar"], ["bk4"])
            ts(T.smi[:, 0:12], T.b37[:, 12 * t + 12:12 * t + 24], B[4][:, 0:1], OP.add, None, None, ["b37", "bk4"], ["fi"])
            ts(T.smi[:, 12:24], T.smi[:, 0:12], 2047, OP.bitwise_and, None, None, ["fi"], ["fj"])
            tt(S(4), S(9), T.smi[:, 12:24], OP.min, ["s9", "fj"], ["s4"])
            tt(S(3), S(6), S(4), OP.max, ["s6", "s4"], ["s3"])
            tt(T.cf[:, :], S(0), S(3), OP.min, ["s0", "s3"], ["cf"])
            cp(T.cl[:, :], T.cf[:, :], ["cf"], ["cl"])
            cp(T.xc[:, :], T.X[:, :].indirect(T.cl[:, :]), ["X", "Xp", "cl"], ["xc"])
        if t == 0:
            matrices3()
        act(B[5][:, 0:NP], B[2][:, NP:2 * NP], AF.Identity, ["bk2", "WB"], ["bk5", "wall"], bias=T.WB[:, t:t + 1], scale=-4096.0)
        mm(B[3][:, NP:2 * NP], MB(6), T.oneh[:, :], True, False, ["MB", "oneh"], ["bk3"])
        mm(B[3][:, NP:2 * NP], MB(1), T.K1[:, :], False, False, ["MB", "K1"], ["bk3"])

    dma("S", "ox", T.yx[:, :], T.X[:, 0:3072], ["X"], [])
    lists()
    turn2(V - 1)
    card_c(V - 1)
    turned()
    ts(T.oya[:, :], T.Tc[:, :], 1536.0, OP.add, None, None, ["Tc"], ["oya"])
    ts(T.IH[:, 0:NP], T.Tc[:, :], EMPTY, OP.is_lt, None, None, ["Tc"], ["inv"])
    tt(T.oyt[:, :], T.oya[:, :], T.IH[:, 0:NP], OP.mult, ["oya", "inv"], ["oyt"])
    dma("S", "ot", T.yt[:, :], T.oyt[:, :], ["oyt"], [])
    card_c2(V - 1)
    tt(B[5][:, NP:2 * NP], B[5][:, NP:2 * NP], T.Hp[:, :], OP.min, ["C1", "bk5", "Hp"], ["bk5", "R3p"])
    hand_end()
    ts(T.IH[:, NP:2 * NP], T.Hs[:, :], EMPTY, OP.is_lt, None, None, ["Hs"], ["hinv"])
    mm(B[1][:, 0:NP], T.UR[:, :], T.Hs[:, :], True, True, ["UR", "Hs"], ["bk1"])
    mm(B[0][0:8, 0:2 * NP], T.M8[:, :], T.IH[:, 0:2 * NP], True, True, ["M8", "inv", "hinv"], ["bk0"])
    ts(T.oyb[:, :], B[1][:, 0:NP], 1536.0, OP.add, None, None, ["bk1"], ["oyb"])
    ts(T.oya[:, :], B[1][:, 0:NP], EMPTY, OP.is_lt, None, None, ["bk1"], ["oya"])
    tt(T.oyh[:, :], T.oya[:, :], T.oyb[:, :], OP.mult, ["oya", "oyb"], ["oyh"])
    dma("S", "oh", T.yh[:, :], T.oyh[:, :], ["oyh"], [])
    cp(T.omn[:, :], B[0][0:8, 0:2 * NP], ["bk0"], ["omn"])
    dma("A", "on", T.yn[:, :], T.omn[:, 0:NP], ["omn"], [])
    dma("A", "om", T.ym[:, :], T.omn[:, NP:2 * NP], ["omn"], [])

    emit(g, core, T, topo, ops, rank)


def emit(g, core, T, topo, ops, rank):
    Q = {"V": g.vector, "A": g.scalar, "P": g.tensor, "G": g, "S": g.sync}
    sems = {"V": "qV", "A": "qA", "P": "qP", "G": "qG"}
    seq, pos = {}, {}
    for k, o in enumerate(ops):
        pos[k] = len(seq.setdefault(o["q"], []))
        seq[o["q"]].append(k)
    know = {q: ({}, set()) for q in "VAPGS"}
    after, needed, waits = {}, set(), {}
    for k, o in enumerate(ops):
        q = o["q"]
        if q == "R":
            after[k] = ({}, set())
            continue
        kn, kd = know[q]
        wl = []

        def learn(d):
            wl.append(d)
            kn2, kd2 = after[d]
            for a in kn2:
                kn[a] = max(kn.get(a, -1), kn2[a])
            kd.update(kd2)

        need = {}
        for d in sorted(o["deps"], reverse=True):
            od = ops[d]
            if not od["dma"]:
                need[od["q"]] = max(need.get(od["q"], -1), pos[d])
            elif d not in kd:
                kd.add(d)
                learn(d)
        for q2 in sorted(need, key=lambda a: -seq[a][need[a]]):
            p = need[q2]
            if kn.get(q2, -1) < p:
                kn[q2] = p
                needed.add(seq[q2][p])
                learn(seq[q2][p])
        waits[k] = wl
        after[k] = (dict(kn), set(kd))
    for q in "VAPG":
        comp = [k for k in seq.get(q, []) if not ops[k]["dma"]]
        if comp:
            needed.add(comp[-1])
    count = {}
    cnt = {q: 0 for q in "VAPG"}
    for k, o in enumerate(ops):
        if k in needed:
            cnt[o["q"]] += 1
            count[k] = cnt[o["q"]]
    n = len(T.cores)
    ein = len(send_engines(topo, T.cores[(rank - 1) % n], core))
    eout = len(send_engines(topo, core, T.cores[(rank + 1) % n]))
    nsend = 0
    for k, o in enumerate(ops):
        q = o["q"]
        if q == "R":
            continue
        e = Q[q]
        for d in waits[k]:
            od = ops[d]
            if od["dma"]:
                e.wait_ge(T.sem[od["dma"]], ein if od["dma"][:3] == "arr" else 16)
            else:
                e.wait_ge(T.sem[sems[od["q"]]], count[d])
        ins = o["f"]()
        if o["dma"] == "snd":
            nsend += 1
        elif o["dma"]:
            ins.then_inc(T.sem[o["dma"]], 16)
        elif k in needed:
            ins.then_inc(T.sem[sems[q]], 1)
    for k, o in enumerate(ops):
        if o["dma"] and o["dma"] != "snd":
            g.wait_ge(T.sem[o["dma"]], ein if o["dma"][:3] == "arr" else 16)
    g.wait_ge(T.sem.snd, eout * nsend)
    for q in "VAPG":
        if cnt[q]:
            g.wait_ge(T.sem[sems[q]], cnt[q])
